import numpy as np, ml_dtypes
CORES = [6,15,38,47]
N = 4
import mx_ref
BF = ml_dtypes.bfloat16
def gcols(t, e):
    v = np.concatenate([t.reshape(8, 16, -1, 4), np.zeros((8, 16, 1, 4), BF)], axis=2)
    return np.ascontiguousarray(np.stack([v[g][:, e[g]] for g in range(8)])).reshape(128, -1)
def tile(rs):
    return np.stack(rs, axis=2).reshape(128, -1).astype(BF)
def pick(q, e):
    c = np.concatenate([q[0].reshape(128, -1, 4), np.zeros((128, 1, 4), np.uint8)], axis=1); s = np.concatenate([q[1], np.ones((16, 1), np.uint8)], axis=1)
    return (np.ascontiguousarray(c[:, e].reshape(128, -1)), np.ascontiguousarray(s[:, e]))
def join(*qs):
    return (np.concatenate([q[0] for q in qs], axis=1), np.concatenate([q[1] for q in qs], axis=1))
def put(q, e, v):
    c, s = q[0].reshape(128, -1, 4).copy(), q[1].copy(); c[:, e] = v[0].reshape(128, -1, 4); s[:, e] = v[1]
    return (c.reshape(128, -1), s)
def pk(c, s):
    return (np.ascontiguousarray(c), mx_ref.live(s))
def emit(q):
    return q[0], q[1]
def packed(v, rng):
    q = [mx_ref.quantize(np.ascontiguousarray(v[r])) for r in range(N)]
    return np.stack([a for a, b in q]), np.stack([mx_ref.plane(b, rng) for a, b in q])
def values_of_codes():
    e, c = np.zeros((128, 128, 4), np.float32), np.zeros((128, 2, 4), np.uint8)
    e[np.arange(128), np.arange(128), 0] = 1
    c[:127, :, 0] = np.arange(256).reshape(2, 128).T[:127]
    return mx_ref.matmul(mx_ref.quantize(e.reshape(128, 512).astype(BF)), (c.reshape(128, 8), np.full((16, 2), 127, np.uint8))).T.reshape(-1).astype(np.float64)
CODE_VALUE, SCALE_VALUE = values_of_codes(), 2.0 ** (np.arange(256) - 127.0)
def decode(q):
    return (CODE_VALUE[q[0]].reshape(16, 8, -1, 4) * SCALE_VALUE[q[1]][:, None, :, None] + 0.0).reshape(128, -1).astype(np.float32)
def f(rng, *shape):
    return mx_ref.flush((rng.standard_normal(shape, dtype=np.float32) * np.exp2(rng.integers(-2, 3, shape[:-1] + (1,)))).astype(BF))
def wide(rng, *shape, cols=0):
    v = rng.standard_normal(shape, dtype=np.float32) * np.exp2(rng.integers(-12, 13, shape)).astype(np.float32)
    if cols: v *= np.repeat(np.exp2(rng.integers(-cols, cols + 1, shape[:-2] + (1, shape[-1] // 4))) * (rng.random(shape[:-2] + (1, shape[-1] // 4)) > 0.0625), 4, axis=-1).astype(np.float32)
    return mx_ref.flush(v.astype(BF))
C, K, R, TEAM = 384, 160, 3, 4
def big(v):
    v = v.astype(np.float32)
    v[np.abs(v) < np.float32(2.0 ** -16)] = 0
    return v.astype(BF)
def numbers_of(rng):
    return {"x": big(f(rng, N, 128, 4 * C)), "u": np.array(f(rng, N, 128, 512)), "v": np.array(f(rng, N, 128, 512))}
def layers(rng):
    return big(f(rng, N, 128, 2048)).reshape(N, 8, 16, 4, 8, 16, 4)
def weights(rng, w):
    c, p = packed(np.ascontiguousarray(w).reshape(N, 128, 2048), rng)
    return {"wc": c, "ws": p}
def setup_inputs(rng):
    return {**numbers_of(rng), **weights(rng, layers(rng))}
def setup_inputs_ties(rng):
    d = numbers_of(rng)
    e = rng.permutation(N)
    x = d["x"].reshape(N, 8, 16, C, 4)
    k = rng.integers(0, 3, (N, 8, 2, C))
    k[:, :, 1] = np.where(rng.random((N, 8, C)) < 0.5, k[:, :, 0], k[:, :, 1])
    x[:, :, :2] = 0
    x[:, :, :2, :, 0] = k.astype(np.float32).astype(BF)
    u = d["u"].reshape(N, 128, 128, 4)
    u[:, :, ::16] = 0
    u[:, :, 1::16] = 0
    for r in range(N):
        for h in range(0, 128, 16):
            for i in range(2): u[r, h + i, h + i, 0] = 0.0 if r == e[0] else -1.0 if r == e[1] else 1.0
    w = layers(rng)
    w[:, :, :, :, :, :2] = 0
    return {"x": x.reshape(N, 128, 4 * C), "u": u.reshape(N, 128, 512), "v": d["v"], **weights(rng, w)}
def setup_inputs_near(rng):
    d = numbers_of(rng)
    x = d["x"].astype(np.float32).reshape(N, 8, 16, C, 4)
    x[:, :, 0] = 0
    x[:, :, 8:] = 0
    x[:, :, 0, :, 0] = rng.integers(0, 2, (N, 8, C)) * 2.0 - 1.0
    for r in range(N):
        for g in rng.permutation(8)[:4]: x[r, g, 0, rng.integers(C), 0] = 2.0 ** 28 * rng.choice([-1.0, 1.0])
    s = rng.integers(0, 16, (N, 8, 2, C))
    for i in range(2): x[:, :, 8 + 2 * i] = ((s[:, :, i, :, None] >> np.arange(4)) & 1) * np.exp2(np.arange(4) - 26.0)
    x[:, :, 11, :, 0] = 2.0 ** -13
    x[:, :, 12, :, 0] = (rng.integers(0, 2, (N, 8, C)) * 2.0 - 1.0) * 2.0 ** -27
    u = d["u"].reshape(N, 128, 128, 4)
    u[:, :, ::16] = 0
    u[:, :, 1::16] = 0
    o = rng.permutation(N) % 4
    for r in range(N):
        k = (1.0, 2.0 ** -30, 2.0 ** -33, 2.0 ** 20)[o[r]]
        for h in range(0, 128, 16):
            if o[r] != 2:
                u[r, h, h:h + 2, 0] = k
                u[r, h + 11, h:h + 2, 0] = 8 * k
            else:
                u[r, h + 12, h, 0] = 8 * k
                u[r, h + 12, h + 1, 0] = 9 * k
            u[r, h + 8, h] = 8 * k
            u[r, h + 10, h + 1] = 8 * k
    w = layers(rng)
    for i in [0, 8, 9, 10, 11, 12, 13, 14, 15]:
        w[:, :, i] = 0
        w[:, :, :, :, :, i] = 0
    return {"x": x.reshape(N, 128, 4 * C).astype(BF), "u": u.reshape(N, 128, 512), "v": d["v"], **weights(rng, w)}
def setup_inputs_sides(rng):
    d = numbers_of(rng)
    x = d["x"].reshape(N, 8, 16, C, 4)
    h = rng.permutation(8)
    j = int(rng.integers(80, C // 2 - 15))
    a = rng.integers(0, 2, (N, 8, C)) * 2.0 - 1.0
    q = min(128, C // 2 - 30)
    for r in range(N):
        a[r, h[0]] = 1.0
        a[r, h[1]] = -1.0
        a[r, h[2]] = 1.0 if r % 2 == 1 else -1.0
        a[r, h[3]] = -1.0 if r % 2 == 1 else 1.0
        a[r, h[4]] = np.where(np.arange(C) < j, 1.0, -1.0)
        a[r, h[5]] = np.where(np.arange(C) < j, -1.0, 1.0)
        a[r, h[6]] = 1.0 if r % TEAM == 0 else np.where((np.arange(C) + r) % 3 == 0, 1.0, -1.0)
        a[r, h[7], :q] = 1.0
        a[r, h[7], q:q + 16] = np.where((np.arange(16) + r) % TEAM == 0, -1.0, 1.0)
        a[r, h[7], q + 16:2 * q + 24] = -1.0
    x[:, :, 0] = 0
    x[:, :, 0, :, 0] = a.astype(np.float32).astype(BF)
    k = (N, 8, 8, C, 4)
    x[:, :, 8:] = ((2 * rng.integers(0, 8, k) + 1) * np.exp2(-rng.integers(11, 15, k).astype(np.float32)) * (rng.integers(0, 2, k) * 2 - 1)).astype(np.float32).astype(BF)
    x[:, :, 8, :, 0] = 1.96875
    u = d["u"].reshape(N, 128, 128, 4)
    u[:, :, ::16] = 0
    u[:, :, 1::16] = 0
    for i in range(0, 128, 16): u[:, i, i, 0] = 1.0
    w = layers(rng)
    w[:, :, :, :, :, 8:] = 0
    return {"x": x.reshape(N, 128, 4 * C), "u": u.reshape(N, 128, 512), "v": d["v"], **weights(rng, w)}
def setup_inputs_huge(rng):
    d = numbers_of(rng)
    c = rng.integers(0, 2, (N, 1, 1, C, 1)) * 2.0 - 1.0
    x = 1.75 * 2.0 ** 27 * (0.75 + 0.25 * rng.random((N, 8, 16, C, 4))) * c
    a = np.full((8, 16, 8, 2, 4), 2.0 ** 30, np.float32)
    for g in range(8):
        a[(g + 1) % 8, :, g, 0] *= 0.5
        a[g, :, g, 1] *= 0.5
    u = d["u"].reshape(N, 128, 8, 16, 4)
    u[:, :, :, :2] = a.reshape(128, 8, 2, 4).astype(BF)
    w = (layers(rng).astype(np.float32) * np.float32(2.0 ** -8)).astype(BF)
    return {"x": x.astype(np.float32).reshape(N, 128, 4 * C).astype(BF), "u": u.reshape(N, 128, 512), "v": d["v"], **weights(rng, w)}
def setup_inputs_spread(rng):
    d = setup_inputs(rng)
    d["x"] = big(wide(rng, N, 128, 4 * C, cols=6))
    return d
def check_inputs(d):
    b = []
    for k in ("x", "u", "v"):
        a = np.abs(d[k].astype(np.float32))
        if not (np.isfinite(a).all() and ((a == 0) | (a >= 2.0 ** -30) & (a <= 2.0 ** 30)).all()): b.append("a value of " + k)
    none, least, most = [emit(mx_ref.quantize(np.full((128, 16), k, np.float32).astype(BF)))[1][0, 0] for k in (0.0, 2.0 ** -30, 2.0 ** 30)]
    for r in range(N):
        if ((d["wc"][r] == 0x7F) | (d["wc"][r] == 0xFF)).any(): b.append("wc: a code that is no number")
        s = mx_ref.live(d["ws"][r])
        if ((s != none) & ((s < least) | (s > most))).any(): b.append("ws: a scale out of range")
    return b
def reference(x, u, v, wc, ws):
    qu = [mx_ref.quantize(u[r]) for r in range(N)]
    lay = [pk(wc[r], ws[r]) for r in range(N)]
    now = [x[r] for r in range(N)]
    order = np.zeros((N, 8, C), np.int64)
    for t in range(R):
        vote = np.zeros((N, 8, C), np.int64)
        for r in range(N):
            s = mx_ref.matmul(qu[r], mx_ref.quantize(now[r]))
            vote[r] = np.where(s[::16] >= s[1::16], 1, -1)
        for m in range(0, N, TEAM):
            a = vote[m:m + TEAM].transpose(1, 2, 0).reshape(8, C * TEAM)
            standing = np.cumsum(a, axis=1) - a
            leaves = ((standing >= 0) == (a > 0)).reshape(8, C, TEAM).transpose(2, 0, 1)
            order[m:m + TEAM] = np.argsort(np.where(leaves, 2 * C - np.arange(C), np.arange(C)), axis=2, kind="stable")
        came = [decode(mx_ref.quantize(gcols(now[r], order[r][:, C - K:]))).astype(BF) for r in range(N)]
        made = []
        for r in range(N):
            b = np.concatenate([came[r - 1], gcols(now[r], order[r][:, :C - K])], axis=1).astype(np.float32)
            z = (b - np.roll(b, 2 * C, axis=1) * np.float32(0.5)).astype(BF)
            q = mx_ref.quantize(z)
            made.append(tile([mx_ref.matmul(pick(lay[r], np.arange(128 * i, 128 * i + 128)), q) * np.float32(0.03125) + z[:, i::4].astype(np.float32) for i in range(4)]))
        now = made
    y, od = np.zeros((N, 128, C), np.float32), np.zeros((N, 8, C), np.float32)
    oc, osc = np.zeros((N, 128, 4 * C), np.uint8), np.zeros((N, 16, C), np.uint8)
    for r in range(N):
        q = mx_ref.quantize(now[r])
        y[r] = mx_ref.matmul(mx_ref.quantize(v[r]), q)
        od[r] = order[r]
        oc[r], osc[r] = emit(q)
    return {"y": y, "od": od, "oc": oc, "osc": osc}

@@ -1,0 +1,378 @@
+from concourse.bass import DstId, RemoteDMATransfer
+from concourse.mybir import dt, AluOpType, ActivationFunctionType
+
+C, K, R, N = 384, 160, 3, 4
+HC = C // 2
+
+SCRATCH = {"ps": ("psum", [128, 4096], "float32")}
+for _d, _t in (
+        ("bfloat16", dict(xt=4 * C, zt=4 * C, z32=4 * C, x32=4 * C, win=8 * C, hb=4 * C, ut=512, vt=512, et=2048, vr=C,
+                          pin=C + 32, tsn=800, d0=HC, m47=48, seg=128, vals=C, sg=48, tb=128, tu=128, no=C + 16,
+                          npv=C + 16, tno=448, tnp=320, sb0=72, sb1=72, sb2=72, lw0=288, lw1=288, lw2=288)),
+        ("float32", dict(s2=C, pf=4, typ=8, z0=4, t24=4, mc=8, la=8, lb=8, lc=8, ld=8, jq=48, kc=48, cj=48, kk=48, uu=48,
+                         ww=48, lv=48, gp=48, ic=128, su=64, sw=64, pl=48, odf=C + 16, ysb=C)),
+        ("int32", dict(idn=128, ul=20, e0=2, pi=4, ek=4, zi=8, zo=8, jw=48)),
+        ("uint16", dict(sl=32, offs=48, lst=32)),
+        ("float8_e4m3fn_x4", dict(qz=C, wq=512, uq=128, u1=128, u2=128, vq=128, eq=512, qx0=C, qx1=C, qx2=C, qx3=C,
+                                  lq0=C, lq1=C, lq2=C)),
+        ("uint8", dict(sz=C, wp=512, us=128, u1s=128, u2s=128, vs=128, es=512, sx0=C, sx1=C, sx2=C, sx3=C,
+                       ls0=C, ls1=C, ls2=C))):
+    for _n, _w in _t.items():
+        SCRATCH[_n] = ("sbuf", [128, _w], _d)
+
+SEMAPHORES = ["cv", "cs", "ct", "cg", "dxa", "dxb", "du", "dw", "dv", "dout", "sent"]
+for _r in range(R):
+    SEMAPHORES += ["av%d" % _r, "aa%d" % _r, "ab%d" % _r, "ap%d" % _r]
+
+
+def rank_program(g, core, T, topo):
+    rank = T.rank_of(core)
+    if rank is None:
+        return
+    A, ACT = AluOpType, ActivationFunctionType
+    cores = list(T.cores)
+    prev, nxt = (rank - 1) % N, (rank + 1) % N
+    others = [m for m in range(N) if m != rank]
+    V, S, Y = g.vector, g.scalar, g.sync
+
+    Q = {"g": g, "v": V, "s": S, "t": g.tensor, "y": Y}
+    own_sem = {"g": "cg", "v": "cv", "s": "cs", "t": "ct"}
+    count, writer, readers = {}, {}, {}
+    clock = {q: {} for q in Q}
+
+    def wait(q, ev):
+        sem, val, clk = ev
+        mine = clock[q]
+        if mine.get(sem, 0) >= val:
+            return
+        Q[q].wait_ge(T.sem[sem], val)
+        mine[sem] = val
+        for s, v in clk.items():
+            if mine.get(s, 0) < v:
+                mine[s] = v
+
+    def op(q, fn, rd=(), wr=(), sem=None, inc=1):
+        need = [writer[t] for t in list(rd) + list(wr) if t in writer]
+        for t in wr:
+            need += readers.get(t, [])
+        for ev in sorted(need, key=lambda e: -e[1]):
+            wait(q, ev)
+        sem = sem or own_sem[q]
+        fn().then_inc(T.sem[sem], inc)
+        count[sem] = count.get(sem, 0) + inc
+        ev = (sem, count[sem], dict(clock[q]))
+        for t in rd:
+            readers.setdefault(t, []).append(ev)
+        for t in wr:
+            writer[t] = ev
+            readers[t] = []
+
+    def arrives(tag, sem, val):
+        writer[tag] = (sem, val, {})
+        count[sem] = val
+
+    def ts(out, in0, s1, op0, rd, wr, s2=None, op1=None):
+        if op1 is None:
+            return op("v", lambda: V.tensor_scalar(out, in0, s1, None, op0), rd, wr)
+        return op("v", lambda: V.tensor_scalar(out, in0, s1, s2, op0, op1), rd, wr)
+
+    def tt(out, in0, in1, o, rd, wr):
+        op("v", lambda: V.tensor_tensor(out, in0, in1, o), rd, wr)
+
+    def cp(out, in_, rd, wr):
+        op("v", lambda: V.tensor_copy(out, in_), rd, wr)
+
+    def ms(ap, val, wr):
+        op("v", lambda: V.memset(ap, val), (), wr)
+
+    def tr(out, in_, rd, wr):
+        op("v", lambda: V.transpose(out, in_), rd, wr)
+
+    def scan(out, d0, d1, init, o0, o1, rd, wr):
+        op("v", lambda: V.tensor_tensor_scan(out, d0, d1, init, o0, o1), rd, wr)
+
+    def act(out, in_, rd, wr, scale=1.0):
+        if scale == 1.0:
+            return op("s", lambda: S.activation(out, in_, ACT.Copy), rd, wr)
+        return op("s", lambda: S.activation(out, in_, ACT.Copy, scale=scale), rd, wr)
+
+    def quant(qb, sb, a, b, src, rd, wr):
+        op("v", lambda: V.quantize_mx(qb[:, a:b], sb[:, a:b], src), rd, wr)
+
+    def mm(k, wq, ws, w0, xq, xs, a, b, rd):
+        op("t", lambda: g.tensor.matmul_mx(T.ps[:, 512 * k:512 * k + b - a], wq[:, w0:w0 + 128], ws[:, w0:w0 + 128],
+                                           xq[:, a:b], xs[:, a:b], True, True), rd, ["p%d" % k])
+
+    def dma(q, out, in_, rd, wr, sem):
+        op(q, lambda: Q[q].dma_start(out, in_), rd, wr, sem, 16)
+
+    def bank(k):
+        return T.ps[:, 512 * k:512 * k + HC]
+
+    def iota(out, pat, base, cm, wr, small=False):
+        if small:
+            return op("g", lambda: g.iota(out, pat, base, cm, allow_small_or_imprecise_dtypes=True), (), wr)
+        return op("g", lambda: g.iota(out, pat, base, cm), (), wr)
+
+    def width(mask):
+        return bin(mask).count("1")
+
+    def send(out, in_, sem, rd):
+        for t in rd:
+            wait("g", writer[t])
+        rid, pid = topo.addr(cores[nxt])[:2]
+        m = topo.mask(core, cores[nxt])
+        g.remote_dma(out, in_, T.sem[sem], T.sem.sent, pid, rid, m)
+        count["sent"] = count.get("sent", 0) + width(m)
+
+    def all_mask(src):
+        m = None
+        for o in range(N):
+            if o != src:
+                x = topo.mask(cores[src], cores[o])
+                m = x if m is None else m & x
+        return m
+
+    def slot(sender, receiver):
+        return [m for m in range(N) if m != receiver].index(sender)
+
+    def four(name):
+        return [name % t for t in range(4)]
+
+    for r in range(R):
+        n_prev = width(topo.mask(cores[prev], core))
+        arrives("lqa%d" % r, "aa%d" % r, n_prev)
+        arrives("lqb%d" % r, "ab%d" % r, n_prev)
+        arrives("ls%d" % r, "ap%d" % r, n_prev)
+        arrives("lw%d" % r, "av%d" % r, sum(width(all_mask(o)) for o in others))
+
+    dma("s", T.ut[:], T.u[:], (), ["ut"], "du")
+    dma("y", T.xt[:, 0:768], T.x[:, 0:768], (), ["xt0"], "dxa")
+    dma("y", T.xt[:, 768:1536], T.x[:, 768:1536], (), ["xt1"], "dxb")
+    wait("y", writer["lqb0"])
+    dma("y", T.wq[:].bitcast(dt.uint8), T.wc[:], (), [], "dw")
+    dma("y", T.wp[:], T.ws[:], (), ["w"], "dw")
+    dma("y", T.vt[:], T.v[:], (), ["vt"], "dv")
+
+    iota(T.ul[:, 0:16], [[1, 2], [16, 8]], 0, 0, ["ul0"])
+    iota(T.e0[:], [[1, 2]], 0, 1, ["e0"])
+    iota(T.ek[:], [[16, 4]], 0, 0, ["ek"])
+    iota(T.ul[:, 16:20], [[16, 4]], 15, 0, ["ul1"])
+    iota(T.idn[:], [[-1, 128]], 0, 1, ["idn"])
+    iota(T.jw[:], [[0, 2], [16, 24]], 0, 0, ["jw"])
+    iota(T.vals[:], [[1, C]], -HC, 0, ["vals"], True)
+
+    pq, ph16, ph, pev = T.pf[:, 0:1], T.pf[:, 1:2], T.pf[:, 2:3], T.pf[:, 3:4]
+    zi = ["zi0", "zi1", "zi2"]
+    ms(T.et[:], 0.0, four("et%d"))
+    cp(T.sl[:, 0:16], T.ul[:, 0:16], ["ul0"], ["slu"])
+    ts(T.pi[:, 0:1], T.e0[:, 0:1], 15, A.bitwise_and, ["e0"], ["pi0"])
+    ts(T.pi[:, 1:2], T.e0[:, 0:1], 16, A.bitwise_and, ["e0"], ["pi1"])
+    ts(T.pi[:, 2:3], T.e0[:, 0:1], 4, A.logical_shift_right, ["e0"], ["pi2"], 1, A.bitwise_and)
+    ts(T.pi[:, 3:4], T.e0[:, 1:2], 1, A.bitwise_and, ["e0"], ["pi3"])
+    ms(T.typ[:], 0.0, ["typ"])
+    ms(T.zi[:], 0, zi)
+    cp(T.pf[:], T.pi[:], four("pi%d"), ["pf"])
+    ms(T.d0[:], 1.0, ["d0"])
+    ms(T.pin[:, 0:16], 0.0, ["pin0"])
+    ms(T.pin[:, 400:416], 0.0, ["pin1"])
+    quant(T.uq, T.us, 0, 128, T.ut[:], ["ut"], ["uq"])
+    ts(T.typ[:, 0:3], T.ek[:, 0:3], pq, A.add, ["ek", "pf"], ["typ"], 24.0, A.is_ge)
+    for uq, us, a, n in ((T.u2, T.u2s, 8, "u2"), (T.u1, T.u1s, 0, "u1")):
+        cp(uq[:, 0:128].bitcast(dt.uint32), T.uq[:, 0:128].bitcast(dt.uint32).indirect(T.sl[:, a:a + 8]), ["uq", "slu"], [n])
+        act(us[:, 0:128], T.us[:, 0:128].indirect(T.sl[:, a:a + 8]), ["uq", "slu"], [n + "s"])
+
+    def own_group_offsets(step):
+        if step == 0:
+            ts(T.z0[:, 0:3], T.ek[:, 0:3], pq, A.add, ["ek", "pf"], ["z0"], ph, A.subtract)
+            ts(T.t24[:, 0:3], T.typ[:, 0:3], -24.0, A.mult, ["typ"], ["t24"], 1.0, A.add)
+            ts(T.zi[:, 4:5], pq, 13.0, A.min, ["pf"], ["zi1"])
+            ts(T.zi[:, 6:7], pq, -6.0, A.add, ["pf"], ["zi2"], 0.0, A.max)
+            tt(T.zi[:, 0:3], T.z0[:, 0:3], T.t24[:, 0:3], A.add, ["z0", "t24"], ["zi0"])
+            ts(T.d0[:], T.d0[:], pev, A.mult, ["pf"], ["d0"])
+        elif step == 1:
+            ts(T.zo[:], T.zi[:], 1, A.bitwise_and, zi, ["zo"])
+            ts(T.la[:], T.zi[:], 16.0, A.mult, zi + ["pf"], ["la"], ph16, A.add)
+            ms(T.mc[:, 0:4], 400.0, ["mc0"])
+            ms(T.mc[:, 4:6], 208.0, ["mc1"])
+            ms(T.mc[:, 6:8], 144.0, ["mc2"])
+            tt(T.lc[:], T.la[:], T.typ[:], A.add, ["la", "typ"], ["lc"])
+            tt(T.lb[:], T.zo[:], T.mc[:], A.mult, ["zo", "mc0", "mc1", "mc2"], ["lb"])
+        else:
+            tt(T.ld[:], T.lb[:], T.lc[:], A.add, ["lb", "lc"], ["ld"])
+            cp(T.sl[:, 20:28], T.ld[:], ["ld"], ["sll"])
+
+    def late_constants():
+        for b in range(4):
+            ts(T.et[:, 512 * b + b:512 * (b + 1):4], T.idn[:], 0.0, A.is_equal, ["idn"], ["et%d" % b])
+        ms(T.m47[:], 1.0, ["m47"])
+        ms(T.seg[:], 1.0, ["seg"])
+        ms(T.tb[:], 0.0, ["tb0", "tb1"])
+        ts(T.jq[:], T.jw[:], pq, A.add, ["jw", "pf"], ["jq"])
+        quant(T.eq, T.es, 0, 512, T.et[:], four("et%d"), ["eq"])
+        ms(T.m47[:, 23:24], 0.0, ["m47"])
+        ms(T.seg[:, 0:128:16], 0.0, ["seg"])
+        ts(T.kc[:, 0:24], T.jq[:, 0:24], 2.0, A.mult, ["jq"], ["kc0"], prev / 2.0 - 2 * C, A.add)
+        ts(T.kc[:, 24:48], T.jq[:, 24:48], 2.0, A.mult, ["jq"], ["kc1"], rank / 2.0 - 2 * C, A.add)
+        ts(T.cj[:], T.jq[:], -1.0, A.mult, ["jq"], ["cj"], float(C), A.add)
+        cp(T.sl[:, 16:20], T.ul[:, 16:20], ["ul1"], ["slb"])
+        ms(T.no[:], 0.0, ["no"])
+        ms(T.npv[:], 0.0, ["npv"])
+
+    def cols(c):
+        return HC * c, HC * (c + 1)
+
+    def quant_x(r, c):
+        a, b = cols(c)
+        quant(T["qx%d" % r], T["sx%d" % r], a, b, T.xt[:, 4 * a:4 * b], ["xt%d" % c], ["qx%d" % c])
+
+    def scores(r, c):
+        a, b = cols(c)
+        qx, sx = T["qx%d" % r], T["sx%d" % r]
+        mm(2 * c, T.u2, T.u2s, 0, qx, sx, a, b, ["u2", "u2s", "qx%d" % c])
+        mm(2 * c + 1, T.u1, T.u1s, 0, qx, sx, a, b, ["u1", "u1s", "qx%d" % c])
+        act(T.s2[:, a:b], bank(2 * c), [], ["p%d" % (2 * c), "s2%d" % c])
+
+    def votes(c):
+        a, b = cols(c)
+        tt(T.vr[:, a:b], bank(2 * c + 1), T.s2[:, a:b], A.is_ge, ["s2%d" % c], ["p%d" % (2 * c + 1), "vr%d" % c])
+        init = -float(HC) if c == 0 else T.pin[:, 15 + HC:16 + HC]
+        scan(T.pin[:, 16 + a:16 + b], T.d0[:], T.vr[:, a:b], init, A.mult, A.add,
+             ["d0", "vr%d" % c] + (["pin0"] if c else []), ["pin%d" % c])
+        if c == 0:
+            tr(T.tsn[:, 0:192], T.pin[:, 0:192], ["pin0"], ["ts0"])
+            tr(T.tsn[:, 416:608], T.pin[:, 16:208], ["pin0"], ["ts1"])
+        else:
+            tr(T.tsn[:, 192:416], T.pin[:, 192:416], ["pin0", "pin1"], ["ts2"])
+            tr(T.tsn[:, 608:800], T.pin[:, 208:400], ["pin1"], ["ts3"])
+
+    def plane(t, a, b):
+        return T.win[:, 2 * C * t + a:2 * C * t + b]
+
+    def second_half_of_x():
+        ts(T.xt[:, 768:1536], T.x32[:, 768:1536], 0.03125, A.mult, four("x32%d1"), ["xt1"])
+
+    for r in range(R):
+        qx, sx, lq, ls, sb, lw = [T[n % r] for n in ("qx%d", "sx%d", "lq%d", "ls%d", "sb%d", "lw%d")]
+        if r == 0:
+            quant_x(0, 0)
+        send(lq[:, 0:HC].bitcast(dt.uint8), qx[:, 0:HC].bitcast(dt.uint8), "aa%d" % r, ["qx0"])
+        scores(r, 0)
+        if r > 0:
+            second_half_of_x()
+        else:
+            own_group_offsets(0)
+        quant_x(r, 1)
+        scores(r, 1)
+        if r == 0:
+            own_group_offsets(1)
+        votes(0)
+        if r == 0:
+            own_group_offsets(2)
+        votes(1)
+        cp(sb[:, 24:72], T.tsn[:, 0:800].indirect(T.sl[:, 20:23]), four("ts%d") + ["sll"], ["sb1"])
+        tt(sb[:, 0:24], sb[:, 24:48], sb[:, 48:72], A.subtract, ["sb1"], ["sb0"])
+        wait("g", writer["sb0"])
+        m = all_mask(rank)
+        tos = [(rank + d) % N for d in range(1, N)]
+        g.remote_dma_fused([RemoteDMATransfer(
+            dst_ids=[DstId(rid=topo.addr(cores[o])[0], pnc=topo.addr(cores[o])[1]) for o in tos],
+            dma_engine_mask=m, remote_sem=T.sem["av%d" % r], srcs=[sb[:, 0:72]],
+            dsts=[lw[:, 96 * slot(rank, o):96 * slot(rank, o) + 72] for o in tos])], local_sem=T.sem.sent)
+        count["sent"] += width(m)
+        send(ls[:], sx[:], "ap%d" % r, ["qx0", "qx1"])
+        send(lq[:, HC:C].bitcast(dt.uint8), qx[:, HC:C].bitcast(dt.uint8), "ab%d" % r, ["qx1"])
+
+        for t in range(4):
+            act(plane(t, 0, C), T.xt[:, t:4 * C:4], ["xt0", "xt1"], ["wo%d" % t])
+        if r == 0:
+            late_constants()
+        if r == 1:
+            quant(T.vq, T.vs, 0, 128, T.vt[:], ["vt"], ["vq"])
+        for c in range(2):
+            a, b = cols(c)
+            for t in range(4):
+                k = 4 * (1 - c) + t
+                mm(k, T.eq, T.es, 128 * t, lq, ls, a, b, ["eq", "ls%d" % r, ("lqa%d", "lqb%d")[c] % r])
+                act(plane(t, C + a, C + b), bank(k), [], ["p%d" % k, "wp%d%d" % (t, c)])
+
+        def part(buf, base, sender, target):
+            o = base + (24 if sender < target else 0)
+            return buf[:, o:o + 24]
+        vv = 96 * slot(prev, rank) + 48
+        cp(lw[:, vv + 24:vv + 48], sb[:, 48:72], ["sb1"], ["vown"])
+        for i, tg in enumerate((prev, rank)):
+            tt(T.kk[:, 24 * i:24 * i + 24], T.kc[:, 24 * i:24 * i + 24], part(sb, 0, rank, tg), A.subtract,
+               ["kc%d" % i, "sb0", "sb1"], ["kk%d" % i])
+
+        for i, tg in enumerate((prev, rank)):
+            tt(T.uu[:, 24 * i:24 * i + 24], part(lw, 0, others[0], tg), part(lw, 96, others[1], tg), A.add,
+               ["lw%d" % r], ["uu%d" % i])
+            tt(T.ww[:, 24 * i:24 * i + 24], T.kk[:, 24 * i:24 * i + 24], part(lw, 192, others[2], tg), A.subtract,
+               ["lw%d" % r, "kk%d" % i], ["ww%d" % i])
+        tt(T.sg[:], T.uu[:], T.ww[:], A.is_ge, ["uu0", "uu1", "ww0", "ww1"], ["sg"])
+        tt(T.tb[:, 0:48], T.sg[:], lw[:, vv:vv + 48], A.not_equal, ["sg", "vown"], ["tb0"])
+        tt(T.lv[:], T.sg[:], lw[:, vv:vv + 48], A.is_equal, ["sg", "vown"], ["lv"])
+        scan(T.tb[:, 65:112], T.tb[:, 0:47], T.m47[:, 0:47], 0.0, A.add, A.mult, ["tb0", "m47"], ["tb1"])
+        tr(T.tu[:], T.tb[:], ["tb0", "tb1"], ["tu"])
+        tt(T.gp[:], T.lv[:], T.cj[:], A.mult, ["lv", "cj"], ["gp"])
+        scan(T.ic[:], T.seg[:], T.tu[:], 0.0, A.mult, A.add, ["seg", "tu"], ["ic"])
+        tt(T.su[:], T.ic[:, 64:128].indirect(T.sl[:, 16:20]), T.ic[:, 0:64], A.add, ["ic", "slb"], ["su"])
+        tr(T.sw[:], T.su[:], ["su"], ["sw"])
+        tt(T.pl[:], T.sw[:, 0:48], T.gp[:], A.add, ["sw", "gp"], ["pl"])
+        ts(T.offs[:], T.pl[:], ph16, A.add, ["pl", "pf"], ["offs"], -1.0, A.add)
+        cp(T.no[:].indirect(T.offs[:, 24:48]), T.vals[:], ["offs", "vals"], ["no"])
+        tr(T.tno[:, 0:224], T.no[:, 0:224], ["no"], ["tno0"])
+        tr(T.tno[:, 224:448], T.no[:, 16:240], ["no"], ["tno1"])
+        ts(T.lst[:, 16:32], T.tno[:].indirect(T.sl[:, 24:25]), float(HC), A.add, ["tno0", "tno1", "sll"], ["lo"])
+        cp(T.npv[:].indirect(T.offs[:, 0:24]), T.vals[:], ["offs", "vals"], ["npv"])
+        tr(T.tnp[:, 0:160], T.npv[:, 224:384], ["npv"], ["tnp0"])
+        tr(T.tnp[:, 160:320], T.npv[:, 240:400], ["npv"], ["tnp1"])
+        ts(T.lst[:, 0:16], T.tnp[:].indirect(T.sl[:, 26:27]), float(HC + C), A.add, ["tnp0", "tnp1", "sll"], ["lp"])
+
+        def half_of_b(c, t):
+            if c == 1:
+                return plane(t, 0, C).indirect(T.lst[:, 18:30]), ["lo", "wo%d" % t]
+            return plane(t, 0, 2 * C).indirect(T.lst[:, 6:18]), ["lo", "lp", "wo%d" % t, "wp%d0" % t, "wp%d1" % t]
+
+        for c in range(2):
+            for t in range(4):
+                src, rd = half_of_b(1 - c, t)
+                act(T.hb[:, C * t + HC * c:C * t + HC * (c + 1)], src, rd, ["h%d%d" % (t, c)], -0.5)
+        for c in range(2):
+            a, b = cols(c)
+            zs = ["z%d%d" % (t, c) for t in range(4)]
+            for t in range(4):
+                src, rd = half_of_b(c, t)
+                tt(T.zt[:, 4 * a + t:4 * b:4], src, T.hb[:, C * t + a:C * t + b], A.add, rd + ["h%d%d" % (t, c)], [zs[t]])
+            quant(T.qz, T.sz, a, b, T.zt[:, 4 * a:4 * b], zs, ["qz%d" % c])
+            act(T.z32[:, 4 * a:4 * b], T.zt[:, 4 * a:4 * b], zs, ["z32%d" % c], 32.0)
+            for t in range(4):
+                mm(4 * c + t, T.wq, T.wp, 128 * t, T.qz, T.sz, a, b, ["w", "qz%d" % c])
+        for c in range(2):
+            a, b = cols(c)
+            for t in range(4):
+                tt(T.x32[:, 4 * a + t:4 * b:4], bank(4 * c + t), T.z32[:, 4 * a + t:4 * b:4], A.add,
+                   ["z32%d" % c], ["p%d" % (4 * c + t), "x32%d%d" % (t, c)])
+            if c == 0:
+                act(T.xt[:, 0:768], T.x32[:, 0:768], four("x32%d0"), ["xt0"], 0.03125)
+        quant_x(r + 1, 0)
+
+    qx, sx = T["qx%d" % R], T["sx%d" % R]
+    op("s", lambda: S.activation(T.odf[:], T.no[:], ACT.Identity, bias=float(HC)), ["no"], ["odf"])
+    mm(0, T.vq, T.vs, 0, qx, sx, 0, HC, ["vq", "qx0"])
+    second_half_of_x()
+    quant_x(R, 1)
+    mm(2, T.vq, T.vs, 0, qx, sx, HC, C, ["vq", "qx1"])
+    dma("y", T.oc[:, 0:4 * HC], qx[:, 0:HC].bitcast(dt.uint8), ["qx0"], [], "dout")
+    for h in range(2):
+        dma("y", T.od[h:8:2, :], T.odf[16 * h:128:32, 16 * h:16 * h + C], ["odf"], [], "dout")
+    act(T.ysb[:, 0:HC], bank(0), [], ["p0", "y0"])
+    dma("s", T.y[:, 0:HC], T.ysb[:, 0:HC], ["y0"], [], "dout")
+    cp(T.ysb[:, HC:C], bank(2), [], ["p2", "y1"])
+    dma("y", T.oc[:, 4 * HC:4 * C], qx[:, HC:C].bitcast(dt.uint8), ["qx1"], [], "dout")
+    for k in range(4):
+        dma("ys"[k // 2], T.osc[4 * k:4 * k + 4, :], sx[32 * k:32 * k + 4, :], ["qx0", "qx1"], [], "dout")
+    dma("s", T.y[:, HC:C], T.ysb[:, HC:C], ["y1"], [], "dout")
+    for sem, val in count.items():
+        wait("g", (sem, val, {}))

@@ -25,19 +25,23 @@ for _r in range(R):
     SEMAPHORES += ["av%d" % _r, "aa%d" % _r, "ab%d" % _r, "ap%d" % _r]
 
 
+def width(mask):
+    return bin(mask).count("1")
+
+
 def rank_program(g, core, T, topo):
     rank = T.rank_of(core)
+    cores = list(T.cores)
     if rank is None:
         return
     A, ACT = AluOpType, ActivationFunctionType
-    cores = list(T.cores)
     prev, nxt = (rank - 1) % N, (rank + 1) % N
     others = [m for m in range(N) if m != rank]
     V, S, Y = g.vector, g.scalar, g.sync
 
     Q = {"g": g, "v": V, "s": S, "t": g.tensor, "y": Y}
     own_sem = {"g": "cg", "v": "cv", "s": "cs", "t": "ct"}
-    count, writer, readers = {}, {}, {}
+    count, writer, readers = {"sent": 0}, {}, {}
     clock = {q: {} for q in Q}
 
     def wait(q, ev):
@@ -114,16 +118,13 @@ def rank_program(g, core, T, topo):
             return op("g", lambda: g.iota(out, pat, base, cm, allow_small_or_imprecise_dtypes=True), (), wr)
         return op("g", lambda: g.iota(out, pat, base, cm), (), wr)
 
-    def width(mask):
-        return bin(mask).count("1")
-
-    def send(out, in_, sem, rd):
+    def send(rd, src, to, m, sem):
         for t in rd:
             wait("g", writer[t])
-        rid, pid = topo.addr(cores[nxt])[:2]
-        m = topo.mask(core, cores[nxt])
-        g.remote_dma(out, in_, T.sem[sem], T.sem.sent, pid, rid, m)
-        count["sent"] = count.get("sent", 0) + width(m)
+        g.remote_dma_fused([RemoteDMATransfer(
+            dst_ids=[DstId(rid=topo.addr(c)[0], pnc=topo.addr(c)[1]) for c, d in to], dma_engine_mask=m,
+            remote_sem=T.sem[sem], srcs=[src], dsts=[d for c, d in to])], local_sem=T.sem.sent)
+        count["sent"] += width(m)
 
     def all_mask(src):
         m = None
@@ -139,18 +140,20 @@ def rank_program(g, core, T, topo):
     def four(name):
         return [name % t for t in range(4)]
 
+    def raw(view):
+        return view.bitcast(dt.uint8)
+
+    to_next = topo.mask(core, cores[nxt])
     for r in range(R):
-        n_prev = width(topo.mask(cores[prev], core))
-        arrives("lqa%d" % r, "aa%d" % r, n_prev)
-        arrives("lqb%d" % r, "ab%d" % r, n_prev)
-        arrives("ls%d" % r, "ap%d" % r, n_prev)
+        for tag, sem in zip(("lqa%d", "lqb%d", "ls%d"), ("aa%d", "ab%d", "ap%d")):
+            arrives(tag % r, sem % r, width(topo.mask(cores[prev], core)))
         arrives("lw%d" % r, "av%d" % r, sum(width(all_mask(o)) for o in others))
 
     dma("s", T.ut[:], T.u[:], (), ["ut"], "du")
     dma("y", T.xt[:, 0:768], T.x[:, 0:768], (), ["xt0"], "dxa")
     dma("y", T.xt[:, 768:1536], T.x[:, 768:1536], (), ["xt1"], "dxb")
     wait("y", writer["lqb0"])
-    dma("y", T.wq[:].bitcast(dt.uint8), T.wc[:], (), [], "dw")
+    dma("y", raw(T.wq[:]), T.wc[:], (), [], "dw")
     dma("y", T.wp[:], T.ws[:], (), ["w"], "dw")
     dma("y", T.vt[:], T.v[:], (), ["vt"], "dv")
 
@@ -200,7 +203,6 @@ def rank_program(g, core, T, topo):
             tt(T.lb[:], T.zo[:], T.mc[:], A.mult, ["zo", "mc0", "mc1", "mc2"], ["lb"])
         else:
             tt(T.ld[:], T.lb[:], T.lc[:], A.add, ["lb", "lc"], ["ld"])
-            cp(T.sl[:, 20:28], T.ld[:], ["ld"], ["sll"])
 
     def late_constants():
         for b in range(4):
@@ -222,9 +224,11 @@ def rank_program(g, core, T, topo):
     def cols(c):
         return HC * c, HC * (c + 1)
 
+    xtags = (["xt0"], ["xt1", "xt2"])
+
     def quant_x(r, c):
         a, b = cols(c)
-        quant(T["qx%d" % r], T["sx%d" % r], a, b, T.xt[:, 4 * a:4 * b], ["xt%d" % c], ["qx%d" % c])
+        quant(T["qx%d" % r], T["sx%d" % r], a, b, T.xt[:, 4 * a:4 * b], xtags[c], ["qx%d" % c])
 
     def scores(r, c):
         a, b = cols(c)
@@ -249,17 +253,17 @@ def rank_program(g, core, T, topo):
     def plane(t, a, b):
         return T.win[:, 2 * C * t + a:2 * C * t + b]
 
-    def second_half_of_x():
-        ts(T.xt[:, 768:1536], T.x32[:, 768:1536], 0.03125, A.mult, four("x32%d1"), ["xt1"])
+    def most_of_second_half_of_x():
+        ts(T.xt[:, 768:1280], T.x32[:, 768:1280], 0.03125, A.mult, four("x32%d1"), ["xt1"])
 
     for r in range(R):
         qx, sx, lq, ls, sb, lw = [T[n % r] for n in ("qx%d", "sx%d", "lq%d", "ls%d", "sb%d", "lw%d")]
         if r == 0:
             quant_x(0, 0)
-        send(lq[:, 0:HC].bitcast(dt.uint8), qx[:, 0:HC].bitcast(dt.uint8), "aa%d" % r, ["qx0"])
+        send(["qx0"], raw(qx[:, 0:HC]), [(cores[nxt], raw(lq[:, 0:HC]))], to_next, "aa%d" % r)
         scores(r, 0)
         if r > 0:
-            second_half_of_x()
+            most_of_second_half_of_x()
         else:
             own_group_offsets(0)
         quant_x(r, 1)
@@ -270,21 +274,18 @@ def rank_program(g, core, T, topo):
         if r == 0:
             own_group_offsets(2)
         votes(1)
+        if r == 0:
+            cp(T.sl[:, 20:28], T.ld[:], ["ld"], ["sll"])
         cp(sb[:, 24:72], T.tsn[:, 0:800].indirect(T.sl[:, 20:23]), four("ts%d") + ["sll"], ["sb1"])
         tt(sb[:, 0:24], sb[:, 24:48], sb[:, 48:72], A.subtract, ["sb1"], ["sb0"])
-        wait("g", writer["sb0"])
-        m = all_mask(rank)
         tos = [(rank + d) % N for d in range(1, N)]
-        g.remote_dma_fused([RemoteDMATransfer(
-            dst_ids=[DstId(rid=topo.addr(cores[o])[0], pnc=topo.addr(cores[o])[1]) for o in tos],
-            dma_engine_mask=m, remote_sem=T.sem["av%d" % r], srcs=[sb[:, 0:72]],
-            dsts=[lw[:, 96 * slot(rank, o):96 * slot(rank, o) + 72] for o in tos])], local_sem=T.sem.sent)
-        count["sent"] += width(m)
-        send(ls[:], sx[:], "ap%d" % r, ["qx0", "qx1"])
-        send(lq[:, HC:C].bitcast(dt.uint8), qx[:, HC:C].bitcast(dt.uint8), "ab%d" % r, ["qx1"])
+        send(["sb0"], sb[:, 0:72], [(cores[o], lw[:, 96 * slot(rank, o):96 * slot(rank, o) + 72]) for o in tos],
+             all_mask(rank), "av%d" % r)
+        send(["qx0", "qx1"], sx[:], [(cores[nxt], ls[:])], to_next, "ap%d" % r)
+        send(["qx1"], raw(qx[:, HC:C]), [(cores[nxt], raw(lq[:, HC:C]))], to_next, "ab%d" % r)
 
         for t in range(4):
-            act(plane(t, 0, C), T.xt[:, t:4 * C:4], ["xt0", "xt1"], ["wo%d" % t])
+            act(plane(t, 0, C), T.xt[:, t:4 * C:4], ["xt0", "xt1", "xt2"], ["wo%d" % t])
         if r == 0:
             late_constants()
         if r == 1:
@@ -310,67 +311,105 @@ def rank_program(g, core, T, topo):
                ["lw%d" % r], ["uu%d" % i])
             tt(T.ww[:, 24 * i:24 * i + 24], T.kk[:, 24 * i:24 * i + 24], part(lw, 192, others[2], tg), A.subtract,
                ["lw%d" % r, "kk%d" % i], ["ww%d" % i])
-        tt(T.sg[:], T.uu[:], T.ww[:], A.is_ge, ["uu0", "uu1", "ww0", "ww1"], ["sg"])
-        tt(T.tb[:, 0:48], T.sg[:], lw[:, vv:vv + 48], A.not_equal, ["sg", "vown"], ["tb0"])
-        tt(T.lv[:], T.sg[:], lw[:, vv:vv + 48], A.is_equal, ["sg", "vown"], ["lv"])
+        for i in range(2):
+            tt(T.sg[:, 24 * i:24 * i + 24], T.uu[:, 24 * i:24 * i + 24], T.ww[:, 24 * i:24 * i + 24], A.is_ge,
+               ["uu%d" % i, "ww%d" % i], ["sg%d" % i])
+        tt(T.tb[:, 0:48], T.sg[:], lw[:, vv:vv + 48], A.not_equal, ["sg0", "sg1", "vown"], ["tb0"])
+        tt(T.lv[:], T.sg[:], lw[:, vv:vv + 48], A.is_equal, ["sg0", "sg1", "vown"], ["lv"])
         scan(T.tb[:, 65:112], T.tb[:, 0:47], T.m47[:, 0:47], 0.0, A.add, A.mult, ["tb0", "m47"], ["tb1"])
-        tr(T.tu[:], T.tb[:], ["tb0", "tb1"], ["tu"])
+        tr(T.tu[:, 0:64], T.tb[:, 0:64], ["tb0"], ["tu0"])
+        tr(T.tu[:, 64:128], T.tb[:, 64:128], ["tb1"], ["tu1"])
+        scan(T.ic[:, 0:64], T.seg[:, 0:64], T.tu[:, 0:64], 0.0, A.mult, A.add, ["seg", "tu0"], ["ic0"])
+        scan(T.ic[:, 64:128], T.seg[:, 0:64], T.tu[:, 64:128], 0.0, A.mult, A.add, ["seg", "tu1"], ["ic1"])
         tt(T.gp[:], T.lv[:], T.cj[:], A.mult, ["lv", "cj"], ["gp"])
-        scan(T.ic[:], T.seg[:], T.tu[:], 0.0, A.mult, A.add, ["seg", "tu"], ["ic"])
-        tt(T.su[:], T.ic[:, 64:128].indirect(T.sl[:, 16:20]), T.ic[:, 0:64], A.add, ["ic", "slb"], ["su"])
+        tt(T.su[:], T.ic[:, 64:128].indirect(T.sl[:, 16:20]), T.ic[:, 0:64], A.add, ["ic0", "ic1", "slb"], ["su"])
         tr(T.sw[:], T.su[:], ["su"], ["sw"])
         tt(T.pl[:], T.sw[:, 0:48], T.gp[:], A.add, ["sw", "gp"], ["pl"])
         ts(T.offs[:], T.pl[:], ph16, A.add, ["pl", "pf"], ["offs"], -1.0, A.add)
+
+        def half_of_b(c, t, a=0, b=12):
+            if c == 1:
+                return plane(t, 0, C).indirect(T.lst[:, 18 + a:18 + b]), ["lo", "wo%d" % t]
+            return plane(t, 0, 2 * C).indirect(T.lst[:, 6 + a:6 + b]), ["lo", "lp", "wo%d" % t, "wp%d0" % t, "wp%d1" % t]
+
+        def scatter_before(i):
+            cp(T.npv[:].indirect(T.offs[:, 8 * i:8 * i + 8]), T.vals[:, 128 * i:128 * i + 128], ["offs", "vals"], ["npv"])
+
+        def halved_piece(i):
+            src, rd = half_of_b(1, 3, 4 * i, 4 * i + 4)
+            ts(T.hb[:, 3 * C + 64 * i:3 * C + 64 * i + 64], src, -0.5, A.mult, rd, ["hp%d" % i])
+
         cp(T.no[:].indirect(T.offs[:, 24:48]), T.vals[:], ["offs", "vals"], ["no"])
+        scatter_before(0)
         tr(T.tno[:, 0:224], T.no[:, 0:224], ["no"], ["tno0"])
         tr(T.tno[:, 224:448], T.no[:, 16:240], ["no"], ["tno1"])
+        scatter_before(1)
         ts(T.lst[:, 16:32], T.tno[:].indirect(T.sl[:, 24:25]), float(HC), A.add, ["tno0", "tno1", "sll"], ["lo"])
-        cp(T.npv[:].indirect(T.offs[:, 0:24]), T.vals[:], ["offs", "vals"], ["npv"])
+        scatter_before(2)
+        halved_piece(0)
         tr(T.tnp[:, 0:160], T.npv[:, 224:384], ["npv"], ["tnp0"])
         tr(T.tnp[:, 160:320], T.npv[:, 240:400], ["npv"], ["tnp1"])
+        halved_piece(1)
         ts(T.lst[:, 0:16], T.tnp[:].indirect(T.sl[:, 26:27]), float(HC + C), A.add, ["tnp0", "tnp1", "sll"], ["lp"])
-
-        def half_of_b(c, t):
-            if c == 1:
-                return plane(t, 0, C).indirect(T.lst[:, 18:30]), ["lo", "wo%d" % t]
-            return plane(t, 0, 2 * C).indirect(T.lst[:, 6:18]), ["lo", "lp", "wo%d" % t, "wp%d0" % t, "wp%d1" % t]
+        halved_piece(2)
 
         for c in range(2):
-            for t in range(4):
+            for t in range(4 if c else 3):
                 src, rd = half_of_b(1 - c, t)
                 act(T.hb[:, C * t + HC * c:C * t + HC * (c + 1)], src, rd, ["h%d%d" % (t, c)], -0.5)
-        for c in range(2):
+
+        def z_plane(c, t):
             a, b = cols(c)
-            zs = ["z%d%d" % (t, c) for t in range(4)]
-            for t in range(4):
-                src, rd = half_of_b(c, t)
-                tt(T.zt[:, 4 * a + t:4 * b:4], src, T.hb[:, C * t + a:C * t + b], A.add, rd + ["h%d%d" % (t, c)], [zs[t]])
-            quant(T.qz, T.sz, a, b, T.zt[:, 4 * a:4 * b], zs, ["qz%d" % c])
-            act(T.z32[:, 4 * a:4 * b], T.zt[:, 4 * a:4 * b], zs, ["z32%d" % c], 32.0)
+            src, rd = half_of_b(c, t)
+            h = ["hp0", "hp1", "hp2"] if (c, t) == (0, 3) else ["h%d%d" % (t, c)]
+            tt(T.zt[:, 4 * a + t:4 * b:4], src, T.hb[:, C * t + a:C * t + b], A.add, rd + h, ["z%d%d" % (t, c)])
+
+        def z_32(c):
+            a, b = cols(c)
+            act(T.z32[:, 4 * a:4 * b], T.zt[:, 4 * a:4 * b], four("z%d" + str(c)), ["z32%d" % c], 32.0)
+
+        def layer(c):
+            a, b = cols(c)
+            quant(T.qz, T.sz, a, b, T.zt[:, 4 * a:4 * b], four("z%d" + str(c)), ["qz%d" % c])
             for t in range(4):
                 mm(4 * c + t, T.wq, T.wp, 128 * t, T.qz, T.sz, a, b, ["w", "qz%d" % c])
-        for c in range(2):
+
+        def x_plane(c, t):
             a, b = cols(c)
-            for t in range(4):
-                tt(T.x32[:, 4 * a + t:4 * b:4], bank(4 * c + t), T.z32[:, 4 * a + t:4 * b:4], A.add,
-                   ["z32%d" % c], ["p%d" % (4 * c + t), "x32%d%d" % (t, c)])
-            if c == 0:
-                act(T.xt[:, 0:768], T.x32[:, 0:768], four("x32%d0"), ["xt0"], 0.03125)
+            tt(T.x32[:, 4 * a + t:4 * b:4], bank(4 * c + t), T.z32[:, 4 * a + t:4 * b:4], A.add,
+               ["z32%d" % c], ["p%d" % (4 * c + t), "x32%d%d" % (t, c)])
+
+        for t in range(4):
+            z_plane(0, t)
+        z_32(0)
+        z_plane(1, 0)
+        layer(0)
+        for t in range(1, 4):
+            z_plane(1, t)
+        z_32(1)
+        x_plane(0, 0)
+        layer(1)
+        for t in range(1, 4):
+            x_plane(0, t)
+        act(T.xt[:, 0:768], T.x32[:, 0:768], four("x32%d0"), ["xt0"], 0.03125)
+        for t in range(4):
+            x_plane(1, t)
+        act(T.xt[:, 1280:1536], T.x32[:, 1280:1536], four("x32%d1"), ["xt2"], 0.03125)
         quant_x(r + 1, 0)
 
     qx, sx = T["qx%d" % R], T["sx%d" % R]
     op("s", lambda: S.activation(T.odf[:], T.no[:], ACT.Identity, bias=float(HC)), ["no"], ["odf"])
     mm(0, T.vq, T.vs, 0, qx, sx, 0, HC, ["vq", "qx0"])
-    second_half_of_x()
+    most_of_second_half_of_x()
     quant_x(R, 1)
     mm(2, T.vq, T.vs, 0, qx, sx, HC, C, ["vq", "qx1"])
-    dma("y", T.oc[:, 0:4 * HC], qx[:, 0:HC].bitcast(dt.uint8), ["qx0"], [], "dout")
+    dma("y", T.oc[:, 0:4 * HC], raw(qx[:, 0:HC]), ["qx0"], [], "dout")
     for h in range(2):
         dma("y", T.od[h:8:2, :], T.odf[16 * h:128:32, 16 * h:16 * h + C], ["odf"], [], "dout")
     act(T.ysb[:, 0:HC], bank(0), [], ["p0", "y0"])
     dma("s", T.y[:, 0:HC], T.ysb[:, 0:HC], ["y0"], [], "dout")
     cp(T.ysb[:, HC:C], bank(2), [], ["p2", "y1"])
-    dma("y", T.oc[:, 4 * HC:4 * C], qx[:, HC:C].bitcast(dt.uint8), ["qx1"], [], "dout")
+    dma("y", T.oc[:, 4 * HC:4 * C], raw(qx[:, HC:C]), ["qx1"], [], "dout")
     for k in range(4):
         dma("ys"[k // 2], T.osc[4 * k:4 * k + 4, :], sx[32 * k:32 * k + 4, :], ["qx0", "qx1"], [], "dout")
     dma("s", T.y[:, HC:C], T.ysb[:, HC:C], ["y1"], [], "dout")

@@ -3,16 +3,17 @@ from concourse.mybir import dt, AluOpType, ActivationFunctionType
 
 C, K, R, N = 384, 160, 3, 4
 HC = C // 2
+THIRDS, HALVES = (0, 128, 256, C), (0, HC, C)
 
 SCRATCH = {"ps": ("psum", [128, 4096], "float32")}
 for _d, _t in (
         ("bfloat16", dict(xt=4 * C, zt=4 * C, z32=4 * C, x32=4 * C, win=8 * C, hb=4 * C, ut=512, vt=512, et=2048, vr=C,
-                          pin=C + 32, tsn=800, d0=HC, m47=48, seg=128, vals=C, sg=48, tb=128, tu=128, no=C + 16,
-                          npv=C + 16, tno=448, tnp=320, sb0=72, sb1=72, sb2=72, lw0=288, lw1=288, lw2=288)),
-        ("float32", dict(s2=C, pf=4, typ=8, z0=4, t24=4, mc=8, la=8, lb=8, lc=8, ld=8, jq=48, kc=48, cj=48, kk=48, uu=48,
-                         ww=48, lv=48, gp=48, ic=128, su=64, sw=64, pl=48, odf=C + 16, ysb=C)),
-        ("int32", dict(idn=128, ul=20, e0=2, pi=4, ek=4, zi=8, zo=8, jw=48)),
-        ("uint16", dict(sl=32, offs=48, lst=32)),
+                          pin=C, tsn=C, d0=HC, m23=24, inc=64, vals=C, sg=48, vo=48, tb=128, tu=128, pt=128, tw=192,
+                          no=C + 16, npv=C + 16, tno=448, tnp=320, sb0=48, sb1=48, sb2=48, lw0=192, lw1=192, lw2=192)),
+        ("float32", dict(s2=C, pf=8, la=4, lb=2, lc=2, b32=2, jq=24, kc=48, cj=32, kk=48, w1=48, w2=48,
+                         sc=128, lm=64, odf=C + 16, ysb=C)),
+        ("int32", dict(idn=128, ul=16, e0=2, pi=8, zi=2, zo=2, jw=24, rw=32)),
+        ("uint16", dict(sl=16, so=8, offs=64, lst=32)),
         ("float8_e4m3fn_x4", dict(qz=C, wq=512, uq=128, u1=128, u2=128, vq=128, eq=512, qx0=C, qx1=C, qx2=C, qx3=C,
                                   lq0=C, lq1=C, lq2=C)),
         ("uint8", dict(sz=C, wp=512, us=128, u1s=128, u2s=128, vs=128, es=512, sx0=C, sx1=C, sx2=C, sx3=C,
@@ -20,9 +21,9 @@ for _d, _t in (
     for _n, _w in _t.items():
         SCRATCH[_n] = ("sbuf", [128, _w], _d)
 
-SEMAPHORES = ["cv", "cs", "ct", "cg", "dxa", "dxb", "du", "dw", "dv", "dout", "sent"]
+SEMAPHORES = ["cv", "cs", "ct", "cg", "dx0", "dx1", "dx2", "du", "dw", "dv", "dout", "sent"]
 for _r in range(R):
-    SEMAPHORES += ["av%d" % _r, "aa%d" % _r, "ab%d" % _r, "ap%d" % _r]
+    SEMAPHORES += ["aa%d" % _r, "ab%d" % _r, "ap%d" % _r] + ["av%d%d" % (_r, _m) for _m in range(N)]
 
 
 def width(mask):
@@ -36,8 +37,13 @@ def rank_program(g, core, T, topo):
         return
     A, ACT = AluOpType, ActivationFunctionType
     prev, nxt = (rank - 1) % N, (rank + 1) % N
-    others = [m for m in range(N) if m != rank]
     V, S, Y = g.vector, g.scalar, g.sync
+
+    def nearness(m):
+        a, b = topo.chip(core), topo.chip(cores[m])
+        return 2 if topo.mates(a, b) else 1 if topo.same_plane(a, b) else 0
+
+    others = sorted((m for m in range(N) if m != rank), key=nearness)
 
     Q = {"g": g, "v": V, "s": S, "t": g.tensor, "y": Y}
     own_sem = {"g": "cg", "v": "cv", "s": "cs", "t": "ct"}
@@ -56,7 +62,7 @@ def rank_program(g, core, T, topo):
                 mine[s] = v
 
     def op(q, fn, rd=(), wr=(), sem=None, inc=1):
-        need = [writer[t] for t in list(rd) + list(wr) if t in writer]
+        need = [writer[t] for t in rd] + [writer[t] for t in wr if t in writer]
         for t in wr:
             need += readers.get(t, [])
         for ev in sorted(need, key=lambda e: -e[1]):
@@ -110,8 +116,8 @@ def rank_program(g, core, T, topo):
     def dma(q, out, in_, rd, wr, sem):
         op(q, lambda: Q[q].dma_start(out, in_), rd, wr, sem, 16)
 
-    def bank(k):
-        return T.ps[:, 512 * k:512 * k + HC]
+    def bank(k, n):
+        return T.ps[:, 512 * k:512 * k + n]
 
     def iota(out, pat, base, cm, wr, small=False):
         if small:
@@ -134,284 +140,339 @@ def rank_program(g, core, T, topo):
                 m = x if m is None else m & x
         return m
 
-    def slot(sender, receiver):
-        return [m for m in range(N) if m != receiver].index(sender)
-
     def four(name):
         return [name % t for t in range(4)]
 
+    def tags(name, a, b, planes=range(4)):
+        return ["%s%d_%d" % (name, t, c) for t in planes for c in range(a // 64, b // 64)]
+
     def raw(view):
         return view.bitcast(dt.uint8)
+
+    def cuts(r):
+        return HALVES if r else THIRDS
+
+    def runs(r):
+        return range(len(cuts(r)) - 1)
 
     to_next = topo.mask(core, cores[nxt])
     for r in range(R):
         for tag, sem in zip(("lqa%d", "lqb%d", "ls%d"), ("aa%d", "ab%d", "ap%d")):
             arrives(tag % r, sem % r, width(topo.mask(cores[prev], core)))
-        arrives("lw%d" % r, "av%d" % r, sum(width(all_mask(o)) for o in others))
+        for o in others:
+            arrives("lw%d%d" % (r, o), "av%d%d" % (r, o), width(all_mask(o)))
 
-    dma("s", T.ut[:], T.u[:], (), ["ut"], "du")
-    dma("y", T.xt[:, 0:768], T.x[:, 0:768], (), ["xt0"], "dxa")
-    dma("y", T.xt[:, 768:1536], T.x[:, 768:1536], (), ["xt1"], "dxb")
-    wait("y", writer["lqb0"])
+    for p in runs(0):
+        a, b = cuts(0)[p:p + 2]
+        dma("y", T.xt[:, 4 * a:4 * b], T.x[:, 4 * a:4 * b], (), tags("xt", a, b), "dx%d" % p)
+        if p == 0:
+            dma("y", T.ut[:], T.u[:], (), ["ut"], "du")
     dma("y", raw(T.wq[:]), T.wc[:], (), [], "dw")
     dma("y", T.wp[:], T.ws[:], (), ["w"], "dw")
+    wait("y", writer["lqb0"])
     dma("y", T.vt[:], T.v[:], (), ["vt"], "dv")
 
-    iota(T.ul[:, 0:16], [[1, 2], [16, 8]], 0, 0, ["ul0"])
+    iota(T.ul[:], [[1, 2], [16, 8]], 0, 0, ["ul"])
     iota(T.e0[:], [[1, 2]], 0, 1, ["e0"])
-    iota(T.ek[:], [[16, 4]], 0, 0, ["ek"])
-    iota(T.ul[:, 16:20], [[16, 4]], 15, 0, ["ul1"])
     iota(T.idn[:], [[-1, 128]], 0, 1, ["idn"])
-    iota(T.jw[:], [[0, 2], [16, 24]], 0, 0, ["jw"])
+    iota(T.jw[:], [[0, 2], [32, 12]], 0, 0, ["jw"])
+    iota(T.rw[:], [[-1, 32]], C, 0, ["rw"])
     iota(T.vals[:], [[1, C]], -HC, 0, ["vals"], True)
 
-    pq, ph16, ph, pev = T.pf[:, 0:1], T.pf[:, 1:2], T.pf[:, 2:3], T.pf[:, 3:4]
-    zi = ["zi0", "zi1", "zi2"]
+    pq, ph16, ph, even, pr, half, odd = [T.pf[:, i:i + 1] for i in range(7)]
+    p0, p1 = T.e0[:, 0:1], T.e0[:, 1:2]
     ms(T.et[:], 0.0, four("et%d"))
-    cp(T.sl[:, 0:16], T.ul[:, 0:16], ["ul0"], ["slu"])
-    ts(T.pi[:, 0:1], T.e0[:, 0:1], 15, A.bitwise_and, ["e0"], ["pi0"])
-    ts(T.pi[:, 1:2], T.e0[:, 0:1], 16, A.bitwise_and, ["e0"], ["pi1"])
-    ts(T.pi[:, 2:3], T.e0[:, 0:1], 4, A.logical_shift_right, ["e0"], ["pi2"], 1, A.bitwise_and)
-    ts(T.pi[:, 3:4], T.e0[:, 1:2], 1, A.bitwise_and, ["e0"], ["pi3"])
-    ms(T.typ[:], 0.0, ["typ"])
-    ms(T.zi[:], 0, zi)
-    cp(T.pf[:], T.pi[:], four("pi%d"), ["pf"])
+    cp(T.sl[:], T.ul[:], ["ul"], ["sl"])
+    for i, (src, shift, bits) in enumerate(((p0, 0, 15), (p0, 0, 16), (p0, 4, 1), (p1, 0, 1), (p0, 0, 31), (p0, 1, 7),
+                                            (p0, 0, 1))):
+        ts(T.pi[:, i:i + 1], src, shift, A.logical_shift_right, ["e0"], ["pi%d" % i], bits, A.bitwise_and)
     ms(T.d0[:], 1.0, ["d0"])
-    ms(T.pin[:, 0:16], 0.0, ["pin0"])
-    ms(T.pin[:, 400:416], 0.0, ["pin1"])
-    quant(T.uq, T.us, 0, 128, T.ut[:], ["ut"], ["uq"])
-    ts(T.typ[:, 0:3], T.ek[:, 0:3], pq, A.add, ["ek", "pf"], ["typ"], 24.0, A.is_ge)
-    for uq, us, a, n in ((T.u2, T.u2s, 8, "u2"), (T.u1, T.u1s, 0, "u1")):
-        cp(uq[:, 0:128].bitcast(dt.uint32), T.uq[:, 0:128].bitcast(dt.uint32).indirect(T.sl[:, a:a + 8]), ["uq", "slu"], [n])
-        act(us[:, 0:128], T.us[:, 0:128].indirect(T.sl[:, a:a + 8]), ["uq", "slu"], [n + "s"])
+    cp(T.pf[:, 0:7], T.pi[:, 0:7], ["pi%d" % i for i in range(7)], ["pf"])
+    ms(T.tb[:], 0.0, four("tb%d"))
+    ts(T.d0[:], T.d0[:], even, A.mult, ["pf"], ["d0"])
+    ms(T.pt[:], 0.0, ["pt0", "pt1"])
 
-    def own_group_offsets(step):
-        if step == 0:
-            ts(T.z0[:, 0:3], T.ek[:, 0:3], pq, A.add, ["ek", "pf"], ["z0"], ph, A.subtract)
-            ts(T.t24[:, 0:3], T.typ[:, 0:3], -24.0, A.mult, ["typ"], ["t24"], 1.0, A.add)
-            ts(T.zi[:, 4:5], pq, 13.0, A.min, ["pf"], ["zi1"])
-            ts(T.zi[:, 6:7], pq, -6.0, A.add, ["pf"], ["zi2"], 0.0, A.max)
-            tt(T.zi[:, 0:3], T.z0[:, 0:3], T.t24[:, 0:3], A.add, ["z0", "t24"], ["zi0"])
-            ts(T.d0[:], T.d0[:], pev, A.mult, ["pf"], ["d0"])
-        elif step == 1:
-            ts(T.zo[:], T.zi[:], 1, A.bitwise_and, zi, ["zo"])
-            ts(T.la[:], T.zi[:], 16.0, A.mult, zi + ["pf"], ["la"], ph16, A.add)
-            ms(T.mc[:, 0:4], 400.0, ["mc0"])
-            ms(T.mc[:, 4:6], 208.0, ["mc1"])
-            ms(T.mc[:, 6:8], 144.0, ["mc2"])
-            tt(T.lc[:], T.la[:], T.typ[:], A.add, ["la", "typ"], ["lc"])
-            tt(T.lb[:], T.zo[:], T.mc[:], A.mult, ["zo", "mc0", "mc1", "mc2"], ["lb"])
-        else:
-            tt(T.ld[:], T.lb[:], T.lc[:], A.add, ["lb", "lc"], ["ld"])
+    def quant_u():
+        quant(T.uq, T.us, 0, 128, T.ut[:], ["ut"], ["uq"])
+        ms(T.m23[:], 1.0, ["m23"])
+        for uq, us, a, n in ((T.u2, T.u2s, 8, "u2"), (T.u1, T.u1s, 0, "u1")):
+            cp(uq[:, 0:128].bitcast(dt.uint32), T.uq[:, 0:128].bitcast(dt.uint32).indirect(T.sl[:, a:a + 8]),
+               ["uq", "sl"], [n])
+            act(us[:, 0:128], T.us[:, 0:128].indirect(T.sl[:, a:a + 8]), ["uq", "sl"], [n + "s"])
 
     def late_constants():
+        ts(T.zi[:, 0:1], pq, 13.0, A.min, ["pf"], ["zi0"])
+        ts(T.zi[:, 1:2], pq, -6.0, A.add, ["pf"], ["zi1"], 0.0, A.max)
+        ts(T.la[:, 0:1], odd, 96.0, A.mult, ["pf"], ["la0"], -52.0, A.add)
+        ts(T.la[:, 1:2], odd, -32.0, A.mult, ["pf"], ["la1"], half, A.add)
+        ts(T.la[:, 2:3], pr, 12.0, A.is_ge, ["pf"], ["la2"], -12.0, A.mult)
+        ts(T.jq[:], T.jw[:], pr, A.add, ["jw", "pf"], ["jq"])
+        ts(T.zo[:], T.zi[:], 1, A.bitwise_and, ["zi0", "zi1"], ["zo"])
+        ts(T.lb[:], T.zi[:], 16.0, A.mult, ["zi0", "zi1", "pf"], ["lb"], ph16, A.add)
+        ts(T.lc[:, 0:1], T.la[:, 0:1], ph, A.mult, ["la0", "la1", "pf"], ["lc"], T.la[:, 1:2], A.add)
+        ts(T.b32[:, 0:1], T.la[:, 2:3], pr, A.add, ["la2", "pf"], ["b0"], 32.0, A.mult)
+        ts(T.kc[:, 0:24], T.jq[:], 2.0, A.mult, ["jq"], ["kc0"], rank / 2.0 - 2 * C, A.add)
+        ts(T.kc[:, 24:48], T.jq[:], 2.0, A.mult, ["jq"], ["kc1"], prev / 2.0 - 2 * C, A.add)
+        ts(T.so[:, 2:3], T.zo[:, 0:1], 208.0, A.mult, ["zo", "lb"], ["so2"], T.lb[:, 0:1], A.add)
+        ts(T.so[:, 4:5], T.zo[:, 1:2], 144.0, A.mult, ["zo", "lb"], ["so4"], T.lb[:, 1:2], A.add)
+        ts(T.so[:, 0:1], T.lc[:, 0:1], 64.0, A.add, ["lc"], ["so0"])
+        ts(T.so[:, 1:2], T.lc[:, 0:1], 72.0, A.add, ["lc"], ["so1"])
+        ts(T.b32[:, 1:2], T.b32[:, 0:1], -1.0 - HC, A.add, ["b0"], ["b1"])
+        ts(T.cj[:], T.rw[:], T.b32[:, 0:1], A.subtract, ["rw", "b0"], ["cj"])
+        ms(T.m23[:, 11:12], 0.0, ["m23"])
+        ms(T.inc[:, 0:32], 0.0, ["inc0"])
+        ms(T.inc[:, 32:64], 1.0, ["inc1"])
         for b in range(4):
             ts(T.et[:, 512 * b + b:512 * (b + 1):4], T.idn[:], 0.0, A.is_equal, ["idn"], ["et%d" % b])
-        ms(T.m47[:], 1.0, ["m47"])
-        ms(T.seg[:], 1.0, ["seg"])
-        ms(T.tb[:], 0.0, ["tb0", "tb1"])
-        ts(T.jq[:], T.jw[:], pq, A.add, ["jw", "pf"], ["jq"])
-        quant(T.eq, T.es, 0, 512, T.et[:], four("et%d"), ["eq"])
-        ms(T.m47[:, 23:24], 0.0, ["m47"])
-        ms(T.seg[:, 0:128:16], 0.0, ["seg"])
-        ts(T.kc[:, 0:24], T.jq[:, 0:24], 2.0, A.mult, ["jq"], ["kc0"], prev / 2.0 - 2 * C, A.add)
-        ts(T.kc[:, 24:48], T.jq[:, 24:48], 2.0, A.mult, ["jq"], ["kc1"], rank / 2.0 - 2 * C, A.add)
-        ts(T.cj[:], T.jq[:], -1.0, A.mult, ["jq"], ["cj"], float(C), A.add)
-        cp(T.sl[:, 16:20], T.ul[:, 16:20], ["ul1"], ["slb"])
         ms(T.no[:], 0.0, ["no"])
+        quant(T.eq, T.es, 0, 512, T.et[:], four("et%d"), ["eq"])
         ms(T.npv[:], 0.0, ["npv"])
 
-    def cols(c):
-        return HC * c, HC * (c + 1)
-
-    xtags = (["xt0"], ["xt1", "xt2"])
-
-    def quant_x(r, c):
-        a, b = cols(c)
-        quant(T["qx%d" % r], T["sx%d" % r], a, b, T.xt[:, 4 * a:4 * b], xtags[c], ["qx%d" % c])
-
-    def scores(r, c):
-        a, b = cols(c)
+    def quant_x(r, p):
+        a, b = cuts(r)[p:p + 2]
         qx, sx = T["qx%d" % r], T["sx%d" % r]
-        mm(2 * c, T.u2, T.u2s, 0, qx, sx, a, b, ["u2", "u2s", "qx%d" % c])
-        mm(2 * c + 1, T.u1, T.u1s, 0, qx, sx, a, b, ["u1", "u1s", "qx%d" % c])
-        act(T.s2[:, a:b], bank(2 * c), [], ["p%d" % (2 * c), "s2%d" % c])
+        quant(qx, sx, a, b, T.xt[:, 4 * a:4 * b], tags("xt", a, b), ["qx%d" % p])
+        if r == R:
+            dma("y", T.oc[:, 4 * a:4 * b], raw(qx[:, a:b]), ["qx%d" % p], [], "dout")
+        elif p == 0:
+            send(["qx0"], raw(qx[:, a:b]), [(cores[nxt], raw(T["lq%d" % r][:, a:b]))], to_next, "aa%d" % r)
 
-    def votes(c):
-        a, b = cols(c)
-        tt(T.vr[:, a:b], bank(2 * c + 1), T.s2[:, a:b], A.is_ge, ["s2%d" % c], ["p%d" % (2 * c + 1), "vr%d" % c])
-        init = -float(HC) if c == 0 else T.pin[:, 15 + HC:16 + HC]
-        scan(T.pin[:, 16 + a:16 + b], T.d0[:], T.vr[:, a:b], init, A.mult, A.add,
-             ["d0", "vr%d" % c] + (["pin0"] if c else []), ["pin%d" % c])
-        if c == 0:
-            tr(T.tsn[:, 0:192], T.pin[:, 0:192], ["pin0"], ["ts0"])
-            tr(T.tsn[:, 416:608], T.pin[:, 16:208], ["pin0"], ["ts1"])
-        else:
-            tr(T.tsn[:, 192:416], T.pin[:, 192:416], ["pin0", "pin1"], ["ts2"])
-            tr(T.tsn[:, 608:800], T.pin[:, 208:400], ["pin1"], ["ts3"])
+    def scores(r, p):
+        a, b = cuts(r)[p:p + 2]
+        qx, sx = T["qx%d" % r], T["sx%d" % r]
+        if r == R:
+            return mm(2 * p, T.vq, T.vs, 0, qx, sx, a, b, ["vq", "qx%d" % p])
+        mm(2 * p, T.u2, T.u2s, 0, qx, sx, a, b, ["u2", "u2s", "qx%d" % p])
+        mm(2 * p + 1, T.u1, T.u1s, 0, qx, sx, a, b, ["u1", "u1s", "qx%d" % p])
+
+    def second_score(r, p):
+        a, b = cuts(r)[p:p + 2]
+        act(T.s2[:, a:b], bank(2 * p, b - a), ["p%d" % (2 * p)], ["s2%d" % p])
+
+    def vote(r, p):
+        a, b = cuts(r)[p:p + 2]
+        tt(T.vr[:, a:b], bank(2 * p + 1, b - a), T.s2[:, a:b], A.is_ge, ["s2%d" % p, "p%d" % (2 * p + 1)], ["vr%d" % p])
+
+    def running_sum(r, p):
+        a, b = cuts(r)[p:p + 2]
+        scan(T.pin[:, a:b], T.d0[:, 0:b - a], T.vr[:, a:b], T.pin[:, a - 1:a] if p else -float(HC), A.mult, A.add,
+             ["d0", "vr%d" % p] + (["pin%d" % (p - 1)] if p else []), ["pin%d" % p])
+
+    def turn(r, p):
+        a, b = cuts(r)[p:p + 2]
+        tr(T.tsn[:, a:b], T.pin[:, a:b], ["pin%d" % p], ["ts%d" % p])
+
+    def sums_of_last_runs(r):
+        p = len(cuts(r)) - 2
+        running_sum(r, p - 1)
+        vote(r, p)
+        turn(r, p - 1)
+        running_sum(r, p)
+        turn(r, p)
+
+    def y_out(p, q, copy):
+        a, b = cuts(R)[p:p + 2]
+        copy(T.ysb[:, a:b], bank(2 * p, b - a), ["p%d" % (2 * p)], ["y%d" % p])
+        dma(q, T.y[:, a:b], T.ysb[:, a:b], ["y%d" % p], [], "dout")
 
     def plane(t, a, b):
         return T.win[:, 2 * C * t + a:2 * C * t + b]
 
-    def most_of_second_half_of_x():
-        ts(T.xt[:, 768:1280], T.x32[:, 768:1280], 0.03125, A.mult, four("x32%d1"), ["xt1"])
+    def of_b(t, c):
+        if c == 1:
+            return plane(t, 0, C).indirect(T.lst[:, 18:30]), ["lo", "wo%d" % t]
+        return plane(t, 0, 2 * C).indirect(T.lst[:, 6:18]), ["lo", "lp", "wo%d" % t, "wp%d0" % t, "wp%d1" % t]
+
+    def at(t, c):
+        return slice(4 * HC * c + t, 4 * HC * (c + 1), 4)
+
+    def named(name, t, c):
+        return tags(name, HC * c, HC * (c + 1), [t])
+
+    def halved(t, c):
+        src, rd = of_b(t, 1 - c)
+        act(T.hb[:, at(t, c)], src, rd, named("h", t, c), -0.5)
+
+    def z_plane(t, c):
+        src, rd = of_b(t, c)
+        tt(T.zt[:, at(t, c)], src, T.hb[:, at(t, c)], A.add, rd + named("h", t, c), named("z", t, c))
+
+    def z_32(t, c):
+        act(T.z32[:, at(t, c)], T.zt[:, at(t, c)], named("z", t, c), named("zz", t, c), 32.0)
+
+    def layer(c):
+        a, b = HALVES[c:c + 2]
+        quant(T.qz, T.sz, a, b, T.zt[:, 4 * a:4 * b], tags("z", a, b), ["qz%d" % c])
+        for t in range(4):
+            mm(4 * c + t, T.wq, T.wp, 128 * t, T.qz, T.sz, a, b, ["w", "qz%d" % c])
+
+    def x_32(t, c):
+        tt(T.x32[:, at(t, c)], bank(4 * c + t, HC), T.z32[:, at(t, c)], A.add,
+           named("zz", t, c) + ["p%d" % (4 * c + t)], named("xx", t, c))
+
+    def x_plane(t, c):
+        if (t, c) == (3, 1):
+            ts(T.xt[:, at(t, c)], T.x32[:, at(t, c)], 0.03125, A.mult, named("xx", t, c), named("xt", t, c))
+        else:
+            act(T.xt[:, at(t, c)], T.x32[:, at(t, c)], named("xx", t, c), named("xt", t, c), 0.03125)
+
+    for p in runs(0):
+        quant_x(0, p)
+        if p == 0:
+            quant_u()
+        scores(0, p)
+        second_score(0, p)
+        if p == 1:
+            vote(0, 0)
+    running_sum(0, 0)
+    vote(0, 1)
+    turn(0, 0)
+    sums_of_last_runs(0)
 
     for r in range(R):
         qx, sx, lq, ls, sb, lw = [T[n % r] for n in ("qx%d", "sx%d", "lq%d", "ls%d", "sb%d", "lw%d")]
-        if r == 0:
-            quant_x(0, 0)
-        send(["qx0"], raw(qx[:, 0:HC]), [(cores[nxt], raw(lq[:, 0:HC]))], to_next, "aa%d" % r)
-        scores(r, 0)
-        if r > 0:
-            most_of_second_half_of_x()
-        else:
-            own_group_offsets(0)
-        quant_x(r, 1)
-        scores(r, 1)
-        if r == 0:
-            own_group_offsets(1)
-        votes(0)
-        if r == 0:
-            own_group_offsets(2)
-        votes(1)
-        if r == 0:
-            cp(T.sl[:, 20:28], T.ld[:], ["ld"], ["sll"])
-        cp(sb[:, 24:72], T.tsn[:, 0:800].indirect(T.sl[:, 20:23]), four("ts%d") + ["sll"], ["sb1"])
-        tt(sb[:, 0:24], sb[:, 24:48], sb[:, 48:72], A.subtract, ["sb1"], ["sb0"])
-        tos = [(rank + d) % N for d in range(1, N)]
-        send(["sb0"], sb[:, 0:72], [(cores[o], lw[:, 96 * slot(rank, o):96 * slot(rank, o) + 72]) for o in tos],
-             all_mask(rank), "av%d" % r)
-        send(["qx0", "qx1"], sx[:], [(cores[nxt], ls[:])], to_next, "ap%d" % r)
-        send(["qx1"], raw(qx[:, HC:C]), [(cores[nxt], raw(lq[:, HC:C]))], to_next, "ab%d" % r)
+        ahead = cuts(r)[1]
+        turned = ["ts%d" % p for p in runs(r)]
+        for h in range(2):
+            upto, own_vote = T.tsn[:, 16 * h:C:32], T.tsn[:, 16 * h + 1:C:32]
+            tt(sb[:, 24 + 12 * h:36 + 12 * h], upto, own_vote, A.subtract, turned, ["se%d" % h])
+            act(sb[:, 12 * h:12 + 12 * h], upto, turned, ["si%d" % h])
+        sums = ["se0", "se1", "si0", "si1"]
+        send(sums, sb[:], [(cores[o], lw[:, 48 * rank:48 * rank + 48]) for o in others], all_mask(rank),
+             "av%d%d" % (r, rank))
+        whole = ["qx%d" % p for p in runs(r)]
+        send(whole, sx[:], [(cores[nxt], ls[:])], to_next, "ap%d" % r)
+        send(whole, raw(qx[:, ahead:C]), [(cores[nxt], raw(lq[:, ahead:C]))], to_next, "ab%d" % r)
 
         for t in range(4):
-            act(plane(t, 0, C), T.xt[:, t:4 * C:4], ["xt0", "xt1", "xt2"], ["wo%d" % t])
+            act(plane(t, 0, C), T.xt[:, t:4 * C:4], tags("xt", 0, C, [t]), ["wo%d" % t])
         if r == 0:
             late_constants()
         if r == 1:
             quant(T.vq, T.vs, 0, 128, T.vt[:], ["vt"], ["vq"])
-        for c in range(2):
-            a, b = cols(c)
+        for c, (a, b) in enumerate(((0, ahead), (ahead, C))):
             for t in range(4):
                 k = 4 * (1 - c) + t
                 mm(k, T.eq, T.es, 128 * t, lq, ls, a, b, ["eq", "ls%d" % r, ("lqa%d", "lqb%d")[c] % r])
-                act(plane(t, C + a, C + b), bank(k), [], ["p%d" % k, "wp%d%d" % (t, c)])
+                act(plane(t, C + a, C + b), bank(k, b - a), ["p%d" % k], ["wp%d%d" % (t, c)])
 
-        def part(buf, base, sender, target):
-            o = base + (24 if sender < target else 0)
+        target = (rank, prev)
+
+        def part(buf, base, sender, i):
+            o = base + (0 if sender < target[i] else 24)
             return buf[:, o:o + 24]
-        vv = 96 * slot(prev, rank) + 48
-        cp(lw[:, vv + 24:vv + 48], sb[:, 48:72], ["sb1"], ["vown"])
-        for i, tg in enumerate((prev, rank)):
-            tt(T.kk[:, 24 * i:24 * i + 24], T.kc[:, 24 * i:24 * i + 24], part(sb, 0, rank, tg), A.subtract,
-               ["kc%d" % i, "sb0", "sb1"], ["kk%d" % i])
 
-        for i, tg in enumerate((prev, rank)):
-            tt(T.uu[:, 24 * i:24 * i + 24], part(lw, 0, others[0], tg), part(lw, 96, others[1], tg), A.add,
-               ["lw%d" % r], ["uu%d" % i])
-            tt(T.ww[:, 24 * i:24 * i + 24], T.kk[:, 24 * i:24 * i + 24], part(lw, 192, others[2], tg), A.subtract,
-               ["lw%d" % r, "kk%d" % i], ["ww%d" % i])
+        def n24(buf, i):
+            return buf[:, 24 * i:24 * i + 24]
+
+        def landed(m):
+            return "lw%d%d" % (r, m)
+
+        def votes_before(m):
+            if m == prev:
+                tt(n24(T.vo, 1), lw[:, 48 * m:48 * m + 24], lw[:, 48 * m + 24:48 * m + 48], A.subtract, [landed(m)], ["vo1"])
+
+        tt(n24(T.vo, 0), sb[:, 0:24], sb[:, 24:48], A.subtract, sums, ["vo0"])
         for i in range(2):
-            tt(T.sg[:, 24 * i:24 * i + 24], T.uu[:, 24 * i:24 * i + 24], T.ww[:, 24 * i:24 * i + 24], A.is_ge,
-               ["uu%d" % i, "ww%d" % i], ["sg%d" % i])
-        tt(T.tb[:, 0:48], T.sg[:], lw[:, vv:vv + 48], A.not_equal, ["sg0", "sg1", "vown"], ["tb0"])
-        tt(T.lv[:], T.sg[:], lw[:, vv:vv + 48], A.is_equal, ["sg0", "sg1", "vown"], ["lv"])
-        scan(T.tb[:, 65:112], T.tb[:, 0:47], T.m47[:, 0:47], 0.0, A.add, A.mult, ["tb0", "m47"], ["tb1"])
-        tr(T.tu[:, 0:64], T.tb[:, 0:64], ["tb0"], ["tu0"])
-        tr(T.tu[:, 64:128], T.tb[:, 64:128], ["tb1"], ["tu1"])
-        scan(T.ic[:, 0:64], T.seg[:, 0:64], T.tu[:, 0:64], 0.0, A.mult, A.add, ["seg", "tu0"], ["ic0"])
-        scan(T.ic[:, 64:128], T.seg[:, 0:64], T.tu[:, 64:128], 0.0, A.mult, A.add, ["seg", "tu1"], ["ic1"])
-        tt(T.gp[:], T.lv[:], T.cj[:], A.mult, ["lv", "cj"], ["gp"])
-        tt(T.su[:], T.ic[:, 64:128].indirect(T.sl[:, 16:20]), T.ic[:, 0:64], A.add, ["ic0", "ic1", "slb"], ["su"])
-        tr(T.sw[:], T.su[:], ["su"], ["sw"])
-        tt(T.pl[:], T.sw[:, 0:48], T.gp[:], A.add, ["sw", "gp"], ["pl"])
-        ts(T.offs[:], T.pl[:], ph16, A.add, ["pl", "pf"], ["offs"], -1.0, A.add)
+            tt(n24(T.kk, i), n24(T.kc, i), part(sb, 0, rank, i), A.subtract, ["kc%d" % i] + sums, ["kk%d" % i])
+        for m, src, dst, sn, dn in ((others[0], T.kk, T.w1, "kk%d", "w1%d"), (others[1], T.w1, T.w2, "w1%d", "w2%d")):
+            for i in range(2):
+                tt(n24(dst, i), n24(src, i), part(lw, 48 * m, m, i), A.subtract, [sn % i, landed(m)], [dn % i])
+            votes_before(m)
 
-        def half_of_b(c, t, a=0, b=12):
-            if c == 1:
-                return plane(t, 0, C).indirect(T.lst[:, 18 + a:18 + b]), ["lo", "wo%d" % t]
-            return plane(t, 0, 2 * C).indirect(T.lst[:, 6 + a:6 + b]), ["lo", "lp", "wo%d" % t, "wp%d0" % t, "wp%d1" % t]
+        def signs(i):
+            m = others[2]
+            tt(n24(T.sg, i), part(lw, 48 * m, m, i), n24(T.w2, i), A.is_ge, [landed(m), "w2%d" % i], ["sg%d" % i])
+            if i == 0:
+                votes_before(m)
 
-        def scatter_before(i):
-            cp(T.npv[:].indirect(T.offs[:, 8 * i:8 * i + 8]), T.vals[:, 128 * i:128 * i + 128], ["offs", "vals"], ["npv"])
+        def leaving(i):
+            tt(T.tb[:, 64 * i + 32:64 * i + 56], n24(T.sg, i), n24(T.vo, i), A.is_equal, ["sg%d" % i, "vo%d" % i],
+               ["tb%d" % (2 * i + 1)])
 
-        def halved_piece(i):
-            src, rd = half_of_b(1, 3, 4 * i, 4 * i + 4)
-            ts(T.hb[:, 3 * C + 64 * i:3 * C + 64 * i + 64], src, -0.5, A.mult, rd, ["hp%d" % i])
+        def earlier_blocks(i):
+            scan(T.tb[:, 64 * i + 1:64 * i + 24], T.tb[:, 64 * i + 32:64 * i + 55], T.m23[:, 0:23], 0.0, A.add, A.mult,
+                 ["tb%d" % (2 * i + 1), "m23"], ["tb%d" % (2 * i)])
 
-        cp(T.no[:].indirect(T.offs[:, 24:48]), T.vals[:], ["offs", "vals"], ["no"])
-        scatter_before(0)
+        def blocks_to_rows(i):
+            tr(T.tu[:, 64 * i:64 * i + 64], T.tb[:, 64 * i:64 * i + 64], ["tb%d" % (2 * i), "tb%d" % (2 * i + 1)],
+               ["tu%d" % i])
+
+        def counts(i):
+            scan(T.sc[:, 64 * i:64 * i + 64], T.inc[:], T.tu[:, 64 * i:64 * i + 64], T.b32[:, 1:2], A.add, A.subtract,
+                 ["inc0", "inc1", "b1", "tu%d" % i], ["sc%d" % i])
+            tt(T.lm[:, 32 * i:32 * i + 32], T.tu[:, 64 * i + 32:64 * i + 64], T.cj[:], A.mult, ["tu%d" % i, "cj"],
+               ["lm%d" % i])
+
+        def places(i):
+            tt(T.pt[:, 64 * i + 16:64 * i + 48], T.sc[:, 64 * i + 32:64 * i + 64], T.lm[:, 32 * i:32 * i + 32], A.add,
+               ["sc%d" % i, "lm%d" % i], ["pt%d" % i])
+
+        def rows_to_groups(i):
+            tr(T.tw[:, 96 * i:96 * i + 64], T.pt[:, 64 * i:64 * i + 64], ["pt%d" % i], ["twa%d" % i])
+            tr(T.tw[:, 96 * i + 64:96 * i + 96], T.pt[:, 64 * i + 16:64 * i + 48], ["pt%d" % i], ["twb%d" % i])
+
+        def offsets(i):
+            ts(T.offs[:, 32 * i:32 * i + 32], T.tw[:, 96 * i:96 * i + 96].indirect(T.so[:, 0:2]), ph16, A.add,
+               ["twa%d" % i, "twb%d" % i, "so0", "so1", "pf"], ["offs%d" % i], float(HC), A.add)
+
+        for step in (signs, leaving, earlier_blocks, blocks_to_rows, counts, places, rows_to_groups, offsets):
+            step(0)
+            step(1)
+
+        def scatter_before(a, b):
+            cp(T.npv[:].indirect(T.offs[:, 32 + a // 16:32 + b // 16]), T.vals[:, a:b], ["offs1", "vals"], ["npv"])
+
+        cp(T.no[:].indirect(T.offs[:, 0:24]), T.vals[:], ["offs0", "vals"], ["no"])
+        scatter_before(0, 32)
         tr(T.tno[:, 0:224], T.no[:, 0:224], ["no"], ["tno0"])
         tr(T.tno[:, 224:448], T.no[:, 16:240], ["no"], ["tno1"])
-        scatter_before(1)
-        ts(T.lst[:, 16:32], T.tno[:].indirect(T.sl[:, 24:25]), float(HC), A.add, ["tno0", "tno1", "sll"], ["lo"])
-        scatter_before(2)
-        halved_piece(0)
+        scatter_before(32, 64)
+        ts(T.lst[:, 16:32], T.tno[:].indirect(T.so[:, 2:3]), float(HC), A.add, ["tno0", "tno1", "so2"], ["lo"])
+        for t in range(4):
+            halved(t, 0)
+        if r == R - 1:
+            op("s", lambda: S.activation(T.odf[:], T.no[:], ACT.Identity, bias=float(HC)), ["no"], ["odf"])
+            for h in range(2):
+                dma("y", T.od[h:8:2, :], T.odf[16 * h:128:32, 16 * h:16 * h + C], ["odf"], [], "dout")
+        scatter_before(64, C)
         tr(T.tnp[:, 0:160], T.npv[:, 224:384], ["npv"], ["tnp0"])
         tr(T.tnp[:, 160:320], T.npv[:, 240:400], ["npv"], ["tnp1"])
-        halved_piece(1)
-        ts(T.lst[:, 0:16], T.tnp[:].indirect(T.sl[:, 26:27]), float(HC + C), A.add, ["tnp0", "tnp1", "sll"], ["lp"])
-        halved_piece(2)
+        ts(T.lst[:, 0:16], T.tnp[:].indirect(T.so[:, 4:5]), float(HC + C), A.add, ["tnp0", "tnp1", "so4"], ["lp"])
 
+        for t in range(4):
+            halved(t, 1)
+            z_plane(t, 0)
+        for t in range(4):
+            z_32(t, 0)
+        for t in range(4):
+            z_plane(t, 1)
+            if t == 0:
+                layer(0)
+            z_32(t, 1)
         for c in range(2):
-            for t in range(4 if c else 3):
-                src, rd = half_of_b(1 - c, t)
-                act(T.hb[:, C * t + HC * c:C * t + HC * (c + 1)], src, rd, ["h%d%d" % (t, c)], -0.5)
-
-        def z_plane(c, t):
-            a, b = cols(c)
-            src, rd = half_of_b(c, t)
-            h = ["hp0", "hp1", "hp2"] if (c, t) == (0, 3) else ["h%d%d" % (t, c)]
-            tt(T.zt[:, 4 * a + t:4 * b:4], src, T.hb[:, C * t + a:C * t + b], A.add, rd + h, ["z%d%d" % (t, c)])
-
-        def z_32(c):
-            a, b = cols(c)
-            act(T.z32[:, 4 * a:4 * b], T.zt[:, 4 * a:4 * b], four("z%d" + str(c)), ["z32%d" % c], 32.0)
-
-        def layer(c):
-            a, b = cols(c)
-            quant(T.qz, T.sz, a, b, T.zt[:, 4 * a:4 * b], four("z%d" + str(c)), ["qz%d" % c])
             for t in range(4):
-                mm(4 * c + t, T.wq, T.wp, 128 * t, T.qz, T.sz, a, b, ["w", "qz%d" % c])
-
-        def x_plane(c, t):
-            a, b = cols(c)
-            tt(T.x32[:, 4 * a + t:4 * b:4], bank(4 * c + t), T.z32[:, 4 * a + t:4 * b:4], A.add,
-               ["z32%d" % c], ["p%d" % (4 * c + t), "x32%d%d" % (t, c)])
-
-        for t in range(4):
-            z_plane(0, t)
-        z_32(0)
-        z_plane(1, 0)
-        layer(0)
-        for t in range(1, 4):
-            z_plane(1, t)
-        z_32(1)
-        x_plane(0, 0)
-        layer(1)
-        for t in range(1, 4):
-            x_plane(0, t)
-        act(T.xt[:, 0:768], T.x32[:, 0:768], four("x32%d0"), ["xt0"], 0.03125)
-        for t in range(4):
-            x_plane(1, t)
-        act(T.xt[:, 1280:1536], T.x32[:, 1280:1536], four("x32%d1"), ["xt2"], 0.03125)
+                x_32(t, c)
+                if (t, c) == (0, 0):
+                    layer(1)
+                if (t, c) != (3, 1):
+                    x_plane(t, c)
         quant_x(r + 1, 0)
+        scores(r + 1, 0)
+        x_plane(3, 1)
+        if r + 1 < R:
+            second_score(r + 1, 0)
+            quant_x(r + 1, 1)
+            scores(r + 1, 1)
+            second_score(r + 1, 1)
+            vote(r + 1, 0)
+            sums_of_last_runs(r + 1)
 
-    qx, sx = T["qx%d" % R], T["sx%d" % R]
-    op("s", lambda: S.activation(T.odf[:], T.no[:], ACT.Identity, bias=float(HC)), ["no"], ["odf"])
-    mm(0, T.vq, T.vs, 0, qx, sx, 0, HC, ["vq", "qx0"])
-    most_of_second_half_of_x()
+    y_out(0, "s", act)
     quant_x(R, 1)
-    mm(2, T.vq, T.vs, 0, qx, sx, HC, C, ["vq", "qx1"])
-    dma("y", T.oc[:, 0:4 * HC], raw(qx[:, 0:HC]), ["qx0"], [], "dout")
-    for h in range(2):
-        dma("y", T.od[h:8:2, :], T.odf[16 * h:128:32, 16 * h:16 * h + C], ["odf"], [], "dout")
-    act(T.ysb[:, 0:HC], bank(0), [], ["p0", "y0"])
-    dma("s", T.y[:, 0:HC], T.ysb[:, 0:HC], ["y0"], [], "dout")
-    cp(T.ysb[:, HC:C], bank(2), [], ["p2", "y1"])
-    dma("y", T.oc[:, 4 * HC:4 * C], raw(qx[:, HC:C]), ["qx1"], [], "dout")
+    scores(R, 1)
     for k in range(4):
-        dma("ys"[k // 2], T.osc[4 * k:4 * k + 4, :], sx[32 * k:32 * k + 4, :], ["qx0", "qx1"], [], "dout")
-    dma("s", T.y[:, HC:C], T.ysb[:, HC:C], ["y1"], [], "dout")
+        dma("ys"[k % 2], T.osc[4 * k:4 * k + 4, :], T["sx%d" % R][32 * k:32 * k + 4, :], ["qx0", "qx1"], [], "dout")
+    y_out(1, "y", cp)
     for sem, val in count.items():
         wait("g", (sem, val, {}))

@@ -2,18 +2,19 @@ from concourse.bass import DstId, RemoteDMATransfer
 from concourse.mybir import dt, AluOpType, ActivationFunctionType
 
 C, K, R, N = 384, 160, 3, 4
-HC = C // 2
+HC, QC = C // 2, C // 4
+BIG = 512.0
 THIRDS, HALVES = (0, 128, 256, C), (0, HC, C)
 
 SCRATCH = {"ps": ("psum", [128, 4096], "float32")}
 for _d, _t in (
-        ("bfloat16", dict(xt=4 * C, zt=4 * C, z32=4 * C, x32=4 * C, win=8 * C, hb=4 * C, ut=512, vt=512, et=2048, vr=C,
-                          pin=C, tsn=C, d0=HC, m23=24, inc=64, vals=C, sg=48, vo=48, tb=128, tu=128, pt=128, tw=192,
-                          no=C + 16, npv=C + 16, tno=448, tnp=320, sb0=48, sb1=48, sb2=48, lw0=192, lw1=192, lw2=192)),
-        ("float32", dict(s2=C, pf=8, la=4, lb=2, lc=2, b32=2, jq=24, kc=48, cj=32, kk=48, w1=48, w2=48,
-                         sc=128, lm=64, odf=C + 16, ysb=C)),
-        ("int32", dict(idn=128, ul=16, e0=2, pi=8, zi=2, zo=2, jw=24, rw=32)),
-        ("uint16", dict(sl=16, so=8, offs=64, lst=32)),
+        ("bfloat16", dict(win=8 * C, zt=4 * C, z32=4 * C, x32=4 * C, hb=4 * C, ut=512, vt=512, et=516, nil=C, vr=C,
+                          pin=C, tsn=C, d0=HC, m23=24, inc=64, vals=C, sg=48, vo=48, sc=128, tb=128, tu=128, pt=128,
+                          tw=192, no=C, npv=C, hold=C - K, h16=48, sb0=48, sb1=48, sb2=48, lw0=192, lw1=192, lw2=192)),
+        ("float32", dict(s2=C, tab=96, pf=96, ca=32, kc=48, cj=32, kk=48, w1=48, w2=48, lm=64, el=4, odf=C, ysb=C)),
+        ("float16", dict(dg=C)),
+        ("int32", dict(idn=128, ul=16)),
+        ("uint16", dict(sl=16, so=2, offs=64, lst=QC, rep=14)),
         ("float8_e4m3fn_x4", dict(qz=C, wq=512, uq=128, u1=128, u2=128, vq=128, eq=512, qx0=C, qx1=C, qx2=C, qx3=C,
                                   lq0=C, lq1=C, lq2=C)),
         ("uint8", dict(sz=C, wp=512, us=128, u1s=128, u2s=128, vs=128, es=512, sx0=C, sx1=C, sx2=C, sx3=C,
@@ -21,9 +22,9 @@ for _d, _t in (
     for _n, _w in _t.items():
         SCRATCH[_n] = ("sbuf", [128, _w], _d)
 
-SEMAPHORES = ["cv", "cs", "ct", "cg", "dx0", "dx1", "dx2", "du", "dw", "dv", "dout", "sent"]
+SEMAPHORES = ["cv", "cs", "ct", "cg", "dx0", "dx1", "dx2", "du", "dw", "dv", "dout", "dod", "dadd", "sent"]
 for _r in range(R):
-    SEMAPHORES += ["aa%d" % _r, "ab%d" % _r, "ap%d" % _r] + ["av%d%d" % (_r, _m) for _m in range(N)]
+    SEMAPHORES += [_s % _r for _s in ("aa%d", "ab%d", "ap%d")] + ["av%d%d" % (_r, _m) for _m in range(N)]
 
 
 def width(mask):
@@ -140,11 +141,8 @@ def rank_program(g, core, T, topo):
                 m = x if m is None else m & x
         return m
 
-    def four(name):
-        return [name % t for t in range(4)]
-
     def tags(name, a, b, planes=range(4)):
-        return ["%s%d_%d" % (name, t, c) for t in planes for c in range(a // 64, b // 64)]
+        return ["%s%d_%d" % (name, t, c) for t in planes for c in range(a // 8, b // 8)]
 
     def raw(view):
         return view.bitcast(dt.uint8)
@@ -162,76 +160,81 @@ def rank_program(g, core, T, topo):
         for o in others:
             arrives("lw%d%d" % (r, o), "av%d%d" % (r, o), width(all_mask(o)))
 
+    dma("y", T.ut[:], T.u[:], (), ["ut"], "du")
     for p in runs(0):
         a, b = cuts(0)[p:p + 2]
-        dma("y", T.xt[:, 4 * a:4 * b], T.x[:, 4 * a:4 * b], (), tags("xt", a, b), "dx%d" % p)
-        if p == 0:
-            dma("y", T.ut[:], T.u[:], (), ["ut"], "du")
+        dma("y", T.win[:, 4 * a:4 * b], T.x[:, 4 * a:4 * b], (), tags("x", a, b), "dx%d" % p)
+    wait("y", writer["lqb0"])
     dma("y", raw(T.wq[:]), T.wc[:], (), [], "dw")
     dma("y", T.wp[:], T.ws[:], (), ["w"], "dw")
-    wait("y", writer["lqb0"])
     dma("y", T.vt[:], T.v[:], (), ["vt"], "dv")
 
     iota(T.ul[:], [[1, 2], [16, 8]], 0, 0, ["ul"])
-    iota(T.e0[:], [[1, 2]], 0, 1, ["e0"])
+    iota(T.tab[:, 0:32], [[0, 8], [1, 4]], 0, 0, ["tab0"], True)
     iota(T.idn[:], [[-1, 128]], 0, 1, ["idn"])
-    iota(T.jw[:], [[0, 2], [32, 12]], 0, 0, ["jw"])
-    iota(T.rw[:], [[-1, 32]], C, 0, ["rw"])
-    iota(T.vals[:], [[1, C]], -HC, 0, ["vals"], True)
+    iota(T.tab[:, 32:64], [[0, 2], [1, 4], [0, 4]], 0, 0, ["tab1"], True)
+    iota(T.tab[:, 64:80], [[1, 8], [-32, 2]], 64, 0, ["tab2"], True)
+    iota(T.tab[:, 80:96], [[1, 8], [64, 2]], 12, 0, ["tab3"], True)
+    element, fourth, turned = [T.pf[:, 32 * i:32 * i + 1] for i in range(3)]
+    first = T.el[:, 2:3]
 
-    pq, ph16, ph, even, pr, half, odd = [T.pf[:, i:i + 1] for i in range(7)]
-    p0, p1 = T.e0[:, 0:1], T.e0[:, 1:2]
-    ms(T.et[:], 0.0, four("et%d"))
+    def affine(out, in_, scale, bias, rd, wr):
+        op("s", lambda: S.activation(out, in_, ACT.Identity, bias=float(bias), scale=float(scale)), rd, wr)
+
+    def quant_e(b):
+        quant(T.eq, T.es, 128 * b, 128 * b + 128, T.et[:, 3 - b:515 - b], ["et"], ["eq%d" % b])
+
+    ms(T.nil[:], 0.0, ["nil"])
+    affine(T.no[:], T.nil[:], 1, 1, ["nil"], ["no"])
+    affine(T.inc[:, 0:32], T.nil[:, 0:32], 1, 0, ["nil"], ["inc0"])
+    affine(T.inc[:, 32:64], T.nil[:, 0:32], 1, 1, ["nil"], ["inc1"])
+    affine(T.tb[:], T.nil[:, 0:128], 1, 0, ["nil"], ["tb0", "tb1", "tb2", "tb3"])
+    affine(T.pt[:], T.nil[:, 0:128], 1, 0, ["nil"], ["pt0", "pt1"])
+    ms(T.et[:], 0.0, ["et"])
     cp(T.sl[:], T.ul[:], ["ul"], ["sl"])
-    for i, (src, shift, bits) in enumerate(((p0, 0, 15), (p0, 0, 16), (p0, 4, 1), (p1, 0, 1), (p0, 0, 31), (p0, 1, 7),
-                                            (p0, 0, 1))):
-        ts(T.pi[:, i:i + 1], src, shift, A.logical_shift_right, ["e0"], ["pi%d" % i], bits, A.bitwise_and)
-    ms(T.d0[:], 1.0, ["d0"])
-    cp(T.pf[:, 0:7], T.pi[:, 0:7], ["pi%d" % i for i in range(7)], ["pf"])
-    ms(T.tb[:], 0.0, four("tb%d"))
-    ts(T.d0[:], T.d0[:], even, A.mult, ["pf"], ["d0"])
-    ms(T.pt[:], 0.0, ["pt0", "pt1"])
+    tr(T.pf[:, 0:32], T.tab[:, 0:32], ["tab0"], ["pe"])
+    ms(T.m23[:], 1.0, ["m23"])
+    ts(T.d0[:], T.nil[:, 0:HC], element, A.is_equal, ["nil", "pe"], ["d0"])
+    ts(T.et[:, 3:515:4], T.idn[:], 0.0, A.is_equal, ["idn"], ["et"])
+    ms(T.m23[:, 11:12], 0.0, ["m23"])
+    quant_e(0)
+    quant_e(1)
 
-    def quant_u():
-        quant(T.uq, T.us, 0, 128, T.ut[:], ["ut"], ["uq"])
-        ms(T.m23[:], 1.0, ["m23"])
-        for uq, us, a, n in ((T.u2, T.u2s, 8, "u2"), (T.u1, T.u1s, 0, "u1")):
-            cp(uq[:, 0:128].bitcast(dt.uint32), T.uq[:, 0:128].bitcast(dt.uint32).indirect(T.sl[:, a:a + 8]),
-               ["uq", "sl"], [n])
-            act(us[:, 0:128], T.us[:, 0:128].indirect(T.sl[:, a:a + 8]), ["uq", "sl"], [n + "s"])
+    quant(T.uq, T.us, 0, 128, T.ut[:], ["ut"], ["uq"])
+
+    def pick_u(n, a):
+        cp(T[n][:, 0:128].bitcast(dt.uint32), T.uq[:, 0:128].bitcast(dt.uint32).indirect(T.sl[:, a:a + 8]),
+           ["uq", "sl"], [n])
+        act(T[n + "s"][:, 0:128], T.us[:, 0:128].indirect(T.sl[:, a:a + 8]), ["uq", "sl"], [n + "s"])
 
     def late_constants():
-        ts(T.zi[:, 0:1], pq, 13.0, A.min, ["pf"], ["zi0"])
-        ts(T.zi[:, 1:2], pq, -6.0, A.add, ["pf"], ["zi1"], 0.0, A.max)
-        ts(T.la[:, 0:1], odd, 96.0, A.mult, ["pf"], ["la0"], -52.0, A.add)
-        ts(T.la[:, 1:2], odd, -32.0, A.mult, ["pf"], ["la1"], half, A.add)
-        ts(T.la[:, 2:3], pr, 12.0, A.is_ge, ["pf"], ["la2"], -12.0, A.mult)
-        ts(T.jq[:], T.jw[:], pr, A.add, ["jw", "pf"], ["jq"])
-        ts(T.zo[:], T.zi[:], 1, A.bitwise_and, ["zi0", "zi1"], ["zo"])
-        ts(T.lb[:], T.zi[:], 16.0, A.mult, ["zi0", "zi1", "pf"], ["lb"], ph16, A.add)
-        ts(T.lc[:, 0:1], T.la[:, 0:1], ph, A.mult, ["la0", "la1", "pf"], ["lc"], T.la[:, 1:2], A.add)
-        ts(T.b32[:, 0:1], T.la[:, 2:3], pr, A.add, ["la2", "pf"], ["b0"], 32.0, A.mult)
-        ts(T.kc[:, 0:24], T.jq[:], 2.0, A.mult, ["jq"], ["kc0"], rank / 2.0 - 2 * C, A.add)
-        ts(T.kc[:, 24:48], T.jq[:], 2.0, A.mult, ["jq"], ["kc1"], prev / 2.0 - 2 * C, A.add)
-        ts(T.so[:, 2:3], T.zo[:, 0:1], 208.0, A.mult, ["zo", "lb"], ["so2"], T.lb[:, 0:1], A.add)
-        ts(T.so[:, 4:5], T.zo[:, 1:2], 144.0, A.mult, ["zo", "lb"], ["so4"], T.lb[:, 1:2], A.add)
-        ts(T.so[:, 0:1], T.lc[:, 0:1], 64.0, A.add, ["lc"], ["so0"])
-        ts(T.so[:, 1:2], T.lc[:, 0:1], 72.0, A.add, ["lc"], ["so1"])
-        ts(T.b32[:, 1:2], T.b32[:, 0:1], -1.0 - HC, A.add, ["b0"], ["b1"])
-        ts(T.cj[:], T.rw[:], T.b32[:, 0:1], A.subtract, ["rw", "b0"], ["cj"])
-        ms(T.m23[:, 11:12], 0.0, ["m23"])
-        ms(T.inc[:, 0:32], 0.0, ["inc0"])
-        ms(T.inc[:, 32:64], 1.0, ["inc1"])
-        for b in range(4):
-            ts(T.et[:, 512 * b + b:512 * (b + 1):4], T.idn[:], 0.0, A.is_equal, ["idn"], ["et%d" % b])
-        ms(T.no[:], 0.0, ["no"])
-        quant(T.eq, T.es, 0, 512, T.et[:], four("et%d"), ["eq"])
-        ms(T.npv[:], 0.0, ["npv"])
+        scan(T.vals[:], T.nil[:], T.no[:], -1.0 - HC, A.add, A.add, ["nil", "no"], ["vals"])
+        tr(T.pf[:, 32:96], T.tab[:, 32:96], ["tab1", "tab2", "tab3"], ["pf"])
+        tr(T.npv[:], T.vals[:], ["vals"], ["npv"])
+        for n in range(4):
+            affine(T.kc[:, 12 * n:12 * n + 12], T.npv[:, 0:C:32], 2, ((rank, prev)[n // 2] + 1) // 2 - C, ["npv"],
+                   ["kc%d" % n])
+        affine(T.ca[:], T.kc[:, 0:32], -0.5, (rank + 1) // 2 / 2.0, ["kc0", "kc1", "kc2"], ["ca"])
+        affine(T.el[:, 0:1], element, 1, 4 * (HC - BIG), ["pe"], ["el0"])
+        affine(T.el[:, 1:2], element, 1, 4 * (HC + C - BIG), ["pe"], ["el1"])
+        ts(T.h16[:, 0:16], T.tab[:, 0:16], fourth, A.is_lt, ["tab0", "pf"], ["h0"], BIG, A.mult)
+        ts(T.h16[:, 16:32], T.tab[:, 0:16], fourth, A.is_equal, ["tab0", "pf"], ["h1"], -BIG, A.mult)
+        ts(T.el[:, 3:4], fourth, 4.0, A.mult, ["pe", "pf"], ["el3"], element, A.add)
+        quant_e(2)
+        tt(T.h16[:, 32:48], T.h16[:, 0:16], T.h16[:, 16:32], A.add, ["h0", "h1"], ["h2"])
+        ts(T.rep[:], T.nil[:, 0:14], T.el[:, 3:4], A.add, ["nil", "el3"], ["rep"])
+        cp(T.so[:, 0:1], turned, ["pf"], ["so0"])
+        ts(T.h16[:, 35:48:4], T.h16[:, 35:48:4], 2 * BIG, A.add, ["h2"], ["h2"])
+        ts(T.so[:, 1:2], turned, 8.0, A.add, ["pf"], ["so1"])
+        quant_e(3)
+        tr(T.cj[:], T.ca[:], ["ca"], ["cj"])
+        affine(first, T.cj[:, 0:1], -1, HC - 1, ["cj"], ["first"])
+        cp(T.hold[:], T.h16[:, 32:48].indirect(T.rep[:]), ["h2", "rep"], ["hold"])
 
     def quant_x(r, p):
         a, b = cuts(r)[p:p + 2]
         qx, sx = T["qx%d" % r], T["sx%d" % r]
-        quant(qx, sx, a, b, T.xt[:, 4 * a:4 * b], tags("xt", a, b), ["qx%d" % p])
+        quant(qx, sx, a, b, T.win[:, 4 * a:4 * b], tags("x", a, b), ["qx%d" % p])
         if r == R:
             dma("y", T.oc[:, 4 * a:4 * b], raw(qx[:, a:b]), ["qx%d" % p], [], "dout")
         elif p == 0:
@@ -244,9 +247,6 @@ def rank_program(g, core, T, topo):
             return mm(2 * p, T.vq, T.vs, 0, qx, sx, a, b, ["vq", "qx%d" % p])
         mm(2 * p, T.u2, T.u2s, 0, qx, sx, a, b, ["u2", "u2s", "qx%d" % p])
         mm(2 * p + 1, T.u1, T.u1s, 0, qx, sx, a, b, ["u1", "u1s", "qx%d" % p])
-
-    def second_score(r, p):
-        a, b = cuts(r)[p:p + 2]
         act(T.s2[:, a:b], bank(2 * p, b - a), ["p%d" % (2 * p)], ["s2%d" % p])
 
     def vote(r, p):
@@ -262,81 +262,66 @@ def rank_program(g, core, T, topo):
         a, b = cuts(r)[p:p + 2]
         tr(T.tsn[:, a:b], T.pin[:, a:b], ["pin%d" % p], ["ts%d" % p])
 
-    def sums_of_last_runs(r):
-        p = len(cuts(r)) - 2
-        running_sum(r, p - 1)
-        vote(r, p)
-        turn(r, p - 1)
-        running_sum(r, p)
-        turn(r, p)
+    def y_out(c, q, copy):
+        a, b = HALVES[c:c + 2]
+        copy(T.ysb[:, a:b], bank(2 * c, HC), ["p%d" % (2 * c)], ["y%d" % c])
+        dma(q, T.y[:, a:b], T.ysb[:, a:b], ["y%d" % c], [], "dout")
 
-    def y_out(p, q, copy):
-        a, b = cuts(R)[p:p + 2]
-        copy(T.ysb[:, a:b], bank(2 * p, b - a), ["p%d" % (2 * p)], ["y%d" % p])
-        dma(q, T.y[:, a:b], T.ysb[:, a:b], ["y%d" % p], [], "dout")
+    def of_b(a, b):
+        lst = T.lst[:, a // 4:b // 4]
+        if a >= K:
+            return T.win[:, 0:4 * C].indirect(lst), ["lo"] + tags("x", 0, C)
+        return T.win[:].indirect(lst), ["lo", "lp"] + tags("x", 0, C) + tags("d", 0, C)
 
-    def plane(t, a, b):
-        return T.win[:, 2 * C * t + a:2 * C * t + b]
+    def halved(a, b):
+        src, rd = of_b((a + HC) % C, (a + HC) % C + b - a)
+        act(T.hb[:, 4 * a:4 * b], src, rd, tags("h", a, b), -0.5)
 
-    def of_b(t, c):
-        if c == 1:
-            return plane(t, 0, C).indirect(T.lst[:, 18:30]), ["lo", "wo%d" % t]
-        return plane(t, 0, 2 * C).indirect(T.lst[:, 6:18]), ["lo", "lp", "wo%d" % t, "wp%d0" % t, "wp%d1" % t]
+    def z_run(a, b):
+        src, rd = of_b(a, b)
+        tt(T.zt[:, 4 * a:4 * b], src, T.hb[:, 4 * a:4 * b], A.add, rd + tags("h", a, b), tags("z", a, b))
 
-    def at(t, c):
-        return slice(4 * HC * c + t, 4 * HC * (c + 1), 4)
-
-    def named(name, t, c):
-        return tags(name, HC * c, HC * (c + 1), [t])
-
-    def halved(t, c):
-        src, rd = of_b(t, 1 - c)
-        act(T.hb[:, at(t, c)], src, rd, named("h", t, c), -0.5)
-
-    def z_plane(t, c):
-        src, rd = of_b(t, c)
-        tt(T.zt[:, at(t, c)], src, T.hb[:, at(t, c)], A.add, rd + named("h", t, c), named("z", t, c))
-
-    def z_32(t, c):
-        act(T.z32[:, at(t, c)], T.zt[:, at(t, c)], named("z", t, c), named("zz", t, c), 32.0)
+    def z_32(a, b):
+        act(T.z32[:, 4 * a:4 * b], T.zt[:, 4 * a:4 * b], tags("z", a, b), tags("zz", a, b), 32.0)
 
     def layer(c):
         a, b = HALVES[c:c + 2]
         quant(T.qz, T.sz, a, b, T.zt[:, 4 * a:4 * b], tags("z", a, b), ["qz%d" % c])
-        for t in range(4):
+        for t in (0, 2, 1, 3):
             mm(4 * c + t, T.wq, T.wp, 128 * t, T.qz, T.sz, a, b, ["w", "qz%d" % c])
 
     def x_32(t, c):
-        tt(T.x32[:, at(t, c)], bank(4 * c + t, HC), T.z32[:, at(t, c)], A.add,
-           named("zz", t, c) + ["p%d" % (4 * c + t)], named("xx", t, c))
+        a, b = HALVES[c:c + 2]
+        tt(T.x32[:, 4 * a + t:4 * b:4], bank(4 * c + t, HC), T.z32[:, 4 * a + t:4 * b:4], A.add,
+           tags("zz", a, b, [t]) + ["p%d" % (4 * c + t)], tags("xx", a, b, [t]))
 
-    def x_plane(t, c):
-        if (t, c) == (3, 1):
-            ts(T.xt[:, at(t, c)], T.x32[:, at(t, c)], 0.03125, A.mult, named("xx", t, c), named("xt", t, c))
+    def new_x(planes, c, on_vector=False):
+        a, b = HALVES[c:c + 2]
+        sl = slice(4 * a + planes[0], 4 * b, 4 // len(planes))
+        if on_vector:
+            ts(T.win[:, sl], T.x32[:, sl], 0.03125, A.mult, tags("xx", a, b, planes), tags("x", a, b, planes))
         else:
-            act(T.xt[:, at(t, c)], T.x32[:, at(t, c)], named("xx", t, c), named("xt", t, c), 0.03125)
+            act(T.win[:, sl], T.x32[:, sl], tags("xx", a, b, planes), tags("x", a, b, planes), 0.03125)
 
+    pick_u("u2", 8)
+    quant_x(0, 0)
+    pick_u("u1", 0)
     for p in runs(0):
-        quant_x(0, p)
-        if p == 0:
-            quant_u()
+        if p:
+            quant_x(0, p)
         scores(0, p)
-        second_score(0, p)
-        if p == 1:
-            vote(0, 0)
-    running_sum(0, 0)
-    vote(0, 1)
-    turn(0, 0)
-    sums_of_last_runs(0)
+    for step, p in ((vote, 0), (running_sum, 0), (vote, 1), (vote, 2), (running_sum, 1), (turn, 0), (running_sum, 2),
+                    (turn, 1), (turn, 2)):
+        step(0, p)
 
     for r in range(R):
         qx, sx, lq, ls, sb, lw = [T[n % r] for n in ("qx%d", "sx%d", "lq%d", "ls%d", "sb%d", "lw%d")]
         ahead = cuts(r)[1]
-        turned = ["ts%d" % p for p in runs(r)]
+        small = ["ts%d" % p for p in runs(r)]
         for h in range(2):
             upto, own_vote = T.tsn[:, 16 * h:C:32], T.tsn[:, 16 * h + 1:C:32]
-            tt(sb[:, 24 + 12 * h:36 + 12 * h], upto, own_vote, A.subtract, turned, ["se%d" % h])
-            act(sb[:, 12 * h:12 + 12 * h], upto, turned, ["si%d" % h])
+            tt(sb[:, 24 + 12 * h:36 + 12 * h], upto, own_vote, A.subtract, small, ["se%d" % h])
+            act(sb[:, 12 * h:12 + 12 * h], upto, small, ["si%d" % h])
         sums = ["se0", "se1", "si0", "si1"]
         send(sums, sb[:], [(cores[o], lw[:, 48 * rank:48 * rank + 48]) for o in others], all_mask(rank),
              "av%d%d" % (r, rank))
@@ -344,45 +329,49 @@ def rank_program(g, core, T, topo):
         send(whole, sx[:], [(cores[nxt], ls[:])], to_next, "ap%d" % r)
         send(whole, raw(qx[:, ahead:C]), [(cores[nxt], raw(lq[:, ahead:C]))], to_next, "ab%d" % r)
 
-        for t in range(4):
-            act(plane(t, 0, C), T.xt[:, t:4 * C:4], tags("xt", 0, C, [t]), ["wo%d" % t])
         if r == 0:
             late_constants()
         if r == 1:
             quant(T.vq, T.vs, 0, 128, T.vt[:], ["vt"], ["vq"])
+            affine(T.odf[:], T.nil[:], 1, HC, ["nil"], ["odf"])
+            dma("s", T.od[:], T.odf[0:8, :], ["odf"], ["od"], "dod")
         for c, (a, b) in enumerate(((0, ahead), (ahead, C))):
             for t in range(4):
                 k = 4 * (1 - c) + t
-                mm(k, T.eq, T.es, 128 * t, lq, ls, a, b, ["eq", "ls%d" % r, ("lqa%d", "lqb%d")[c] % r])
-                act(plane(t, C + a, C + b), bank(k, b - a), ["p%d" % k], ["wp%d%d" % (t, c)])
-
-        target = (rank, prev)
-
-        def part(buf, base, sender, i):
-            o = base + (0 if sender < target[i] else 24)
-            return buf[:, o:o + 24]
+                mm(k, T.eq, T.es, 128 * t, lq, ls, a, b, ["eq%d" % t, "ls%d" % r, ("lqa%d", "lqb%d")[c] % r])
+                act(T.win[:, 4 * (C + a) + t:4 * (C + b):4], bank(k, b - a), ["p%d" % k], tags("d", a, b, [t]))
 
         def n24(buf, i):
             return buf[:, 24 * i:24 * i + 24]
+
+        def n32(buf, i):
+            return buf[:, 32 * i:32 * i + 32]
+
+        def n64(buf, i):
+            return buf[:, 64 * i:64 * i + 64]
+
+        def part(buf, slot, sender, i):
+            return n24(buf, 2 * slot + (0 if sender < (rank, prev)[i] else 1))
 
         def landed(m):
             return "lw%d%d" % (r, m)
 
         def votes_before(m):
             if m == prev:
-                tt(n24(T.vo, 1), lw[:, 48 * m:48 * m + 24], lw[:, 48 * m + 24:48 * m + 48], A.subtract, [landed(m)], ["vo1"])
+                tt(n24(T.vo, 1), n24(lw, 2 * m), n24(lw, 2 * m + 1), A.subtract, [landed(m)], ["vo1"])
 
-        tt(n24(T.vo, 0), sb[:, 0:24], sb[:, 24:48], A.subtract, sums, ["vo0"])
+        tt(n24(T.vo, 0), n24(sb, 0), n24(sb, 1), A.subtract, sums, ["vo0"])
         for i in range(2):
-            tt(n24(T.kk, i), n24(T.kc, i), part(sb, 0, rank, i), A.subtract, ["kc%d" % i] + sums, ["kk%d" % i])
+            tt(n24(T.kk, i), n24(T.kc, i), part(sb, 0, rank, i), A.subtract,
+               ["kc%d" % (2 * i), "kc%d" % (2 * i + 1)] + sums, ["kk%d" % i])
         for m, src, dst, sn, dn in ((others[0], T.kk, T.w1, "kk%d", "w1%d"), (others[1], T.w1, T.w2, "w1%d", "w2%d")):
             for i in range(2):
-                tt(n24(dst, i), n24(src, i), part(lw, 48 * m, m, i), A.subtract, [sn % i, landed(m)], [dn % i])
+                tt(n24(dst, i), n24(src, i), part(lw, m, m, i), A.subtract, [sn % i, landed(m)], [dn % i])
             votes_before(m)
 
         def signs(i):
             m = others[2]
-            tt(n24(T.sg, i), part(lw, 48 * m, m, i), n24(T.w2, i), A.is_ge, [landed(m), "w2%d" % i], ["sg%d" % i])
+            tt(n24(T.sg, i), part(lw, m, m, i), n24(T.w2, i), A.is_ge, [landed(m), "w2%d" % i], ["sg%d" % i])
             if i == 0:
                 votes_before(m)
 
@@ -395,26 +384,24 @@ def rank_program(g, core, T, topo):
                  ["tb%d" % (2 * i + 1), "m23"], ["tb%d" % (2 * i)])
 
         def blocks_to_rows(i):
-            tr(T.tu[:, 64 * i:64 * i + 64], T.tb[:, 64 * i:64 * i + 64], ["tb%d" % (2 * i), "tb%d" % (2 * i + 1)],
-               ["tu%d" % i])
+            tr(n64(T.tu, i), n64(T.tb, i), ["tb%d" % (2 * i), "tb%d" % (2 * i + 1)], ["tu%d" % i])
 
         def counts(i):
-            scan(T.sc[:, 64 * i:64 * i + 64], T.inc[:], T.tu[:, 64 * i:64 * i + 64], T.b32[:, 1:2], A.add, A.subtract,
-                 ["inc0", "inc1", "b1", "tu%d" % i], ["sc%d" % i])
-            tt(T.lm[:, 32 * i:32 * i + 32], T.tu[:, 64 * i + 32:64 * i + 64], T.cj[:], A.mult, ["tu%d" % i, "cj"],
-               ["lm%d" % i])
+            scan(n64(T.sc, i), T.inc[:], n64(T.tu, i), first, A.add, A.subtract, ["inc0", "inc1", "first", "tu%d" % i],
+                 ["sc%d" % i])
+            tt(n32(T.lm, i), n32(T.tu, 2 * i + 1), T.cj[:], A.mult, ["tu%d" % i, "cj"], ["lm%d" % i])
 
         def places(i):
-            tt(T.pt[:, 64 * i + 16:64 * i + 48], T.sc[:, 64 * i + 32:64 * i + 64], T.lm[:, 32 * i:32 * i + 32], A.add,
-               ["sc%d" % i, "lm%d" % i], ["pt%d" % i])
+            tt(T.pt[:, 64 * i + 16:64 * i + 48], n32(T.sc, 2 * i + 1), n32(T.lm, i), A.add, ["sc%d" % i, "lm%d" % i],
+               ["pt%d" % i])
 
         def rows_to_groups(i):
-            tr(T.tw[:, 96 * i:96 * i + 64], T.pt[:, 64 * i:64 * i + 64], ["pt%d" % i], ["twa%d" % i])
+            tr(T.tw[:, 96 * i:96 * i + 64], n64(T.pt, i), ["pt%d" % i], ["twa%d" % i])
             tr(T.tw[:, 96 * i + 64:96 * i + 96], T.pt[:, 64 * i + 16:64 * i + 48], ["pt%d" % i], ["twb%d" % i])
 
         def offsets(i):
-            ts(T.offs[:, 32 * i:32 * i + 32], T.tw[:, 96 * i:96 * i + 96].indirect(T.so[:, 0:2]), ph16, A.add,
-               ["twa%d" % i, "twb%d" % i, "so0", "so1", "pf"], ["offs%d" % i], float(HC), A.add)
+            ts(n32(T.offs, i), T.tw[:, 96 * i:96 * i + 96].indirect(T.so[:]), float(HC), A.add,
+               ["twa%d" % i, "twb%d" % i, "so0", "so1"], ["offs%d" % i])
 
         for step in (signs, leaving, earlier_blocks, blocks_to_rows, counts, places, rows_to_groups, offsets):
             step(0)
@@ -424,55 +411,55 @@ def rank_program(g, core, T, topo):
             cp(T.npv[:].indirect(T.offs[:, 32 + a // 16:32 + b // 16]), T.vals[:, a:b], ["offs1", "vals"], ["npv"])
 
         cp(T.no[:].indirect(T.offs[:, 0:24]), T.vals[:], ["offs0", "vals"], ["no"])
-        scatter_before(0, 32)
-        tr(T.tno[:, 0:224], T.no[:, 0:224], ["no"], ["tno0"])
-        tr(T.tno[:, 224:448], T.no[:, 16:240], ["no"], ["tno1"])
-        scatter_before(32, 64)
-        ts(T.lst[:, 16:32], T.tno[:].indirect(T.so[:, 2:3]), float(HC), A.add, ["tno0", "tno1", "so2"], ["lo"])
-        for t in range(4):
-            halved(t, 0)
         if r == R - 1:
-            op("s", lambda: S.activation(T.odf[:], T.no[:], ACT.Identity, bias=float(HC)), ["no"], ["odf"])
-            for h in range(2):
-                dma("y", T.od[h:8:2, :], T.odf[16 * h:128:32, 16 * h:16 * h + C], ["odf"], [], "dout")
-        scatter_before(64, C)
-        tr(T.tnp[:, 0:160], T.npv[:, 224:384], ["npv"], ["tnp0"])
-        tr(T.tnp[:, 160:320], T.npv[:, 240:400], ["npv"], ["tnp1"])
-        ts(T.lst[:, 0:16], T.tnp[:].indirect(T.so[:, 4:5]), float(HC + C), A.add, ["tnp0", "tnp1", "so4"], ["lp"])
+            op("g", lambda: g.dma_start(T.od[:], T.no[0:128:16, :], accum_op=A.add), ["no", "od"], (), "dadd", 16)
+        scatter_before(0, 32)
+        scan(T.dg[:, 0:C - K], T.no[:, 0:C - K], T.hold[:], BIG, A.min, A.add, ["no", "hold"], ["dg0"])
+        ts(T.lst[:, K // 4:QC], T.dg[:, 3:C - K:4], 4.0, A.mult, ["dg0", "el0"], ["lo"], T.el[:, 0:1], A.add)
+        halved(HC + K, C)
+        halved(0, QC)
+        halved(QC, HC)
+        scatter_before(32, C)
+        z_run(C - 32, C - 24)
+        scan(T.dg[:, C - K:C], T.npv[:, C - K:C], T.hold[:, 0:K], BIG, A.min, A.add, ["npv", "hold"], ["dg1"])
+        z_run(C - 24, C - 8)
+        ts(T.lst[:, 0:K // 4], T.dg[:, C - K + 3:C:4], 4.0, A.mult, ["dg1", "el1"], ["lp"], T.el[:, 1:2], A.add)
+        z_run(C - 8, C)
 
-        for t in range(4):
-            halved(t, 1)
-            z_plane(t, 0)
-        for t in range(4):
-            z_32(t, 0)
-        for t in range(4):
-            z_plane(t, 1)
-            if t == 0:
-                layer(0)
-            z_32(t, 1)
+        mid = HC + K // 2
+        halved(HC, mid)
+        halved(mid, HC + K)
+        z_run(0, QC)
+        z_run(QC, HC)
+        z_32(0, HC)
+        z_run(HC, mid)
+        layer(0)
+        z_run(mid, HC + K)
+        z_32(HC, mid)
+        z_32(mid, C)
         for c in range(2):
-            for t in range(4):
+            for t in (0, 2, 1, 3):
                 x_32(t, c)
                 if (t, c) == (0, 0):
                     layer(1)
-                if (t, c) != (3, 1):
-                    x_plane(t, c)
-        quant_x(r + 1, 0)
-        scores(r + 1, 0)
-        x_plane(3, 1)
+                if (t, c) == (3, 1):
+                    quant_x(r + 1, 0)
+                    scores(r + 1, 0)
+                if t == 2 or (t, c) == (3, 0):
+                    new_x((t - 2, t), c)
+                elif t and c:
+                    new_x((t,), c, t == 3)
         if r + 1 < R:
-            second_score(r + 1, 0)
             quant_x(r + 1, 1)
             scores(r + 1, 1)
-            second_score(r + 1, 1)
-            vote(r + 1, 0)
-            sums_of_last_runs(r + 1)
+            for step, p in ((vote, 0), (running_sum, 0), (vote, 1), (turn, 0), (running_sum, 1), (turn, 1)):
+                step(r + 1, p)
 
     y_out(0, "s", act)
     quant_x(R, 1)
     scores(R, 1)
     for k in range(4):
-        dma("ys"[k % 2], T.osc[4 * k:4 * k + 4, :], T["sx%d" % R][32 * k:32 * k + 4, :], ["qx0", "qx1"], [], "dout")
+        dma("s" if k else "y", T.osc[4 * k:4 * k + 4, :], T["sx%d" % R][32 * k:32 * k + 4, :], ["qx0", "qx1"], [], "dout")
     y_out(1, "y", cp)
     for sem, val in count.items():
         wait("g", (sem, val, {}))

from concourse.bass import DstId, RemoteDMATransfer
from concourse.mybir import dt, AluOpType, ActivationFunctionType

C, K, R, N = 384, 160, 3, 4
HC, QC = C // 2, C // 4
BIG = 512.0
THIRDS, HALVES = (0, 128, 256, C), (0, HC, C)

SCRATCH = {"ps": ("psum", [128, 4096], "float32")}
for _d, _t in (
        ("bfloat16", dict(win=8 * C, zt=4 * C, z32=4 * C, x32=4 * C, hb=4 * C, ut=512, vt=512, et=516, nil=C, vr=C,
                          pin=C, tsn=C, d0=HC, m23=24, inc=64, vals=C, sg=48, vo=48, sc=128, tb=128, tu=128, pt=128,
                          tw=192, no=C, npv=C, hold=C - K, h16=48, sb0=48, sb1=48, sb2=48, lw0=192, lw1=192, lw2=192)),
        ("float32", dict(s2=C, tab=96, pf=96, ca=32, kc=48, cj=32, kk=48, w1=48, w2=48, lm=64, el=4, odf=C, ysb=C)),
        ("float16", dict(dg=C)),
        ("int32", dict(idn=128, ul=16)),
        ("uint16", dict(sl=16, so=2, offs=64, lst=QC, rep=14)),
        ("float8_e4m3fn_x4", dict(qz=C, wq=512, uq=128, u1=128, u2=128, vq=128, eq=512, qx0=C, qx1=C, qx2=C, qx3=C,
                                  lq0=C, lq1=C, lq2=C)),
        ("uint8", dict(sz=C, wp=512, us=128, u1s=128, u2s=128, vs=128, es=512, sx0=C, sx1=C, sx2=C, sx3=C,
                       ls0=C, ls1=C, ls2=C))):
    for _n, _w in _t.items():
        SCRATCH[_n] = ("sbuf", [128, _w], _d)

SEMAPHORES = ["cv", "cs", "ct", "cg", "dx0", "dx1", "dx2", "du", "dw", "dv", "dout", "dod", "dadd", "sent"]
for _r in range(R):
    SEMAPHORES += [_s % _r for _s in ("aa%d", "ab%d", "ap%d")] + ["av%d%d" % (_r, _m) for _m in range(N)]


def width(mask):
    return bin(mask).count("1")


def rank_program(g, core, T, topo):
    rank = T.rank_of(core)
    cores = list(T.cores)
    if rank is None:
        return
    A, ACT = AluOpType, ActivationFunctionType
    prev, nxt = (rank - 1) % N, (rank + 1) % N
    V, S, Y = g.vector, g.scalar, g.sync

    def nearness(m):
        a, b = topo.chip(core), topo.chip(cores[m])
        return 2 if topo.mates(a, b) else 1 if topo.same_plane(a, b) else 0

    others = sorted((m for m in range(N) if m != rank), key=nearness)

    Q = {"g": g, "v": V, "s": S, "t": g.tensor, "y": Y}
    own_sem = {"g": "cg", "v": "cv", "s": "cs", "t": "ct"}
    count, writer, readers = {"sent": 0}, {}, {}
    clock = {q: {} for q in Q}

    def wait(q, ev):
        sem, val, clk = ev
        mine = clock[q]
        if mine.get(sem, 0) >= val:
            return
        Q[q].wait_ge(T.sem[sem], val)
        mine[sem] = val
        for s, v in clk.items():
            if mine.get(s, 0) < v:
                mine[s] = v

    def op(q, fn, rd=(), wr=(), sem=None, inc=1):
        need = [writer[t] for t in rd] + [writer[t] for t in wr if t in writer]
        for t in wr:
            need += readers.get(t, [])
        for ev in sorted(need, key=lambda e: -e[1]):
            wait(q, ev)
        sem = sem or own_sem[q]
        fn().then_inc(T.sem[sem], inc)
        count[sem] = count.get(sem, 0) + inc
        ev = (sem, count[sem], dict(clock[q]))
        for t in rd:
            readers.setdefault(t, []).append(ev)
        for t in wr:
            writer[t] = ev
            readers[t] = []

    def arrives(tag, sem, val):
        writer[tag] = (sem, val, {})
        count[sem] = val

    def ts(out, in0, s1, op0, rd, wr, s2=None, op1=None):
        if op1 is None:
            return op("v", lambda: V.tensor_scalar(out, in0, s1, None, op0), rd, wr)
        return op("v", lambda: V.tensor_scalar(out, in0, s1, s2, op0, op1), rd, wr)

    def tt(out, in0, in1, o, rd, wr):
        op("v", lambda: V.tensor_tensor(out, in0, in1, o), rd, wr)

    def cp(out, in_, rd, wr):
        op("v", lambda: V.tensor_copy(out, in_), rd, wr)

    def ms(ap, val, wr):
        op("v", lambda: V.memset(ap, val), (), wr)

    def tr(out, in_, rd, wr):
        op("v", lambda: V.transpose(out, in_), rd, wr)

    def scan(out, d0, d1, init, o0, o1, rd, wr):
        op("v", lambda: V.tensor_tensor_scan(out, d0, d1, init, o0, o1), rd, wr)

    def act(out, in_, rd, wr, scale=1.0):
        if scale == 1.0:
            return op("s", lambda: S.activation(out, in_, ACT.Copy), rd, wr)
        return op("s", lambda: S.activation(out, in_, ACT.Copy, scale=scale), rd, wr)

    def quant(qb, sb, a, b, src, rd, wr):
        op("v", lambda: V.quantize_mx(qb[:, a:b], sb[:, a:b], src), rd, wr)

    def mm(k, wq, ws, w0, xq, xs, a, b, rd):
        op("t", lambda: g.tensor.matmul_mx(T.ps[:, 512 * k:512 * k + b - a], wq[:, w0:w0 + 128], ws[:, w0:w0 + 128],
                                           xq[:, a:b], xs[:, a:b], True, True), rd, ["p%d" % k])

    def dma(q, out, in_, rd, wr, sem):
        op(q, lambda: Q[q].dma_start(out, in_), rd, wr, sem, 16)

    def bank(k, n):
        return T.ps[:, 512 * k:512 * k + n]

    def iota(out, pat, base, cm, wr, small=False):
        if small:
            return op("g", lambda: g.iota(out, pat, base, cm, allow_small_or_imprecise_dtypes=True), (), wr)
        return op("g", lambda: g.iota(out, pat, base, cm), (), wr)

    def send(rd, src, to, m, sem):
        for t in rd:
            wait("g", writer[t])
        g.remote_dma_fused([RemoteDMATransfer(
            dst_ids=[DstId(rid=topo.addr(c)[0], pnc=topo.addr(c)[1]) for c, d in to], dma_engine_mask=m,
            remote_sem=T.sem[sem], srcs=[src], dsts=[d for c, d in to])], local_sem=T.sem.sent)
        count["sent"] += width(m)

    def all_mask(src):
        m = None
        for o in range(N):
            if o != src:
                x = topo.mask(cores[src], cores[o])
                m = x if m is None else m & x
        return m

    def tags(name, a, b, planes=range(4)):
        return ["%s%d_%d" % (name, t, c) for t in planes for c in range(a // 8, b // 8)]

    def raw(view):
        return view.bitcast(dt.uint8)

    def cuts(r):
        return HALVES if r else THIRDS

    def runs(r):
        return range(len(cuts(r)) - 1)

    to_next = topo.mask(core, cores[nxt])
    for r in range(R):
        for tag, sem in zip(("lqa%d", "lqb%d", "ls%d"), ("aa%d", "ab%d", "ap%d")):
            arrives(tag % r, sem % r, width(topo.mask(cores[prev], core)))
        for o in others:
            arrives("lw%d%d" % (r, o), "av%d%d" % (r, o), width(all_mask(o)))

    dma("y", T.ut[:], T.u[:], (), ["ut"], "du")
    for p in runs(0):
        a, b = cuts(0)[p:p + 2]
        dma("y", T.win[:, 4 * a:4 * b], T.x[:, 4 * a:4 * b], (), tags("x", a, b), "dx%d" % p)
    wait("y", writer["lqb0"])
    dma("y", raw(T.wq[:]), T.wc[:], (), [], "dw")
    dma("y", T.wp[:], T.ws[:], (), ["w"], "dw")
    dma("y", T.vt[:], T.v[:], (), ["vt"], "dv")

    iota(T.ul[:], [[1, 2], [16, 8]], 0, 0, ["ul"])
    iota(T.tab[:, 0:32], [[0, 8], [1, 4]], 0, 0, ["tab0"], True)
    iota(T.idn[:], [[-1, 128]], 0, 1, ["idn"])
    iota(T.tab[:, 32:64], [[0, 2], [1, 4], [0, 4]], 0, 0, ["tab1"], True)
    iota(T.tab[:, 64:80], [[1, 8], [-32, 2]], 64, 0, ["tab2"], True)
    iota(T.tab[:, 80:96], [[1, 8], [64, 2]], 12, 0, ["tab3"], True)
    element, fourth, turned = [T.pf[:, 32 * i:32 * i + 1] for i in range(3)]
    first = T.el[:, 2:3]

    def affine(out, in_, scale, bias, rd, wr):
        op("s", lambda: S.activation(out, in_, ACT.Identity, bias=float(bias), scale=float(scale)), rd, wr)

    def quant_e(b):
        quant(T.eq, T.es, 128 * b, 128 * b + 128, T.et[:, 3 - b:515 - b], ["et"], ["eq%d" % b])

    ms(T.nil[:], 0.0, ["nil"])
    affine(T.no[:], T.nil[:], 1, 1, ["nil"], ["no"])
    affine(T.inc[:, 0:32], T.nil[:, 0:32], 1, 0, ["nil"], ["inc0"])
    affine(T.inc[:, 32:64], T.nil[:, 0:32], 1, 1, ["nil"], ["inc1"])
    affine(T.tb[:], T.nil[:, 0:128], 1, 0, ["nil"], ["tb0", "tb1", "tb2", "tb3"])
    affine(T.pt[:], T.nil[:, 0:128], 1, 0, ["nil"], ["pt0", "pt1"])
    ms(T.et[:], 0.0, ["et"])
    cp(T.sl[:], T.ul[:], ["ul"], ["sl"])
    tr(T.pf[:, 0:32], T.tab[:, 0:32], ["tab0"], ["pe"])
    ms(T.m23[:], 1.0, ["m23"])
    ts(T.d0[:], T.nil[:, 0:HC], element, A.is_equal, ["nil", "pe"], ["d0"])
    ts(T.et[:, 3:515:4], T.idn[:], 0.0, A.is_equal, ["idn"], ["et"])
    ms(T.m23[:, 11:12], 0.0, ["m23"])
    quant_e(0)
    quant_e(1)

    quant(T.uq, T.us, 0, 128, T.ut[:], ["ut"], ["uq"])

    def pick_u(n, a):
        cp(T[n][:, 0:128].bitcast(dt.uint32), T.uq[:, 0:128].bitcast(dt.uint32).indirect(T.sl[:, a:a + 8]),
           ["uq", "sl"], [n])
        act(T[n + "s"][:, 0:128], T.us[:, 0:128].indirect(T.sl[:, a:a + 8]), ["uq", "sl"], [n + "s"])

    def late_constants():
        scan(T.vals[:], T.nil[:], T.no[:], -1.0 - HC, A.add, A.add, ["nil", "no"], ["vals"])
        tr(T.pf[:, 32:96], T.tab[:, 32:96], ["tab1", "tab2", "tab3"], ["pf"])
        tr(T.npv[:], T.vals[:], ["vals"], ["npv"])
        for n in range(4):
            affine(T.kc[:, 12 * n:12 * n + 12], T.npv[:, 0:C:32], 2, ((rank, prev)[n // 2] + 1) // 2 - C, ["npv"],
                   ["kc%d" % n])
        affine(T.ca[:], T.kc[:, 0:32], -0.5, (rank + 1) // 2 / 2.0, ["kc0", "kc1", "kc2"], ["ca"])
        affine(T.el[:, 0:1], element, 1, 4 * (HC - BIG), ["pe"], ["el0"])
        affine(T.el[:, 1:2], element, 1, 4 * (HC + C - BIG), ["pe"], ["el1"])
        ts(T.h16[:, 0:16], T.tab[:, 0:16], fourth, A.is_lt, ["tab0", "pf"], ["h0"], BIG, A.mult)
        ts(T.h16[:, 16:32], T.tab[:, 0:16], fourth, A.is_equal, ["tab0", "pf"], ["h1"], -BIG, A.mult)
        ts(T.el[:, 3:4], fourth, 4.0, A.mult, ["pe", "pf"], ["el3"], element, A.add)
        quant_e(2)
        tt(T.h16[:, 32:48], T.h16[:, 0:16], T.h16[:, 16:32], A.add, ["h0", "h1"], ["h2"])
        ts(T.rep[:], T.nil[:, 0:14], T.el[:, 3:4], A.add, ["nil", "el3"], ["rep"])
        cp(T.so[:, 0:1], turned, ["pf"], ["so0"])
        ts(T.h16[:, 35:48:4], T.h16[:, 35:48:4], 2 * BIG, A.add, ["h2"], ["h2"])
        ts(T.so[:, 1:2], turned, 8.0, A.add, ["pf"], ["so1"])
        quant_e(3)
        tr(T.cj[:], T.ca[:], ["ca"], ["cj"])
        affine(first, T.cj[:, 0:1], -1, HC - 1, ["cj"], ["first"])
        cp(T.hold[:], T.h16[:, 32:48].indirect(T.rep[:]), ["h2", "rep"], ["hold"])

    def quant_x(r, p):
        a, b = cuts(r)[p:p + 2]
        qx, sx = T["qx%d" % r], T["sx%d" % r]
        quant(qx, sx, a, b, T.win[:, 4 * a:4 * b], tags("x", a, b), ["qx%d" % p])
        if r == R:
            dma("y", T.oc[:, 4 * a:4 * b], raw(qx[:, a:b]), ["qx%d" % p], [], "dout")
        elif p == 0:
            send(["qx0"], raw(qx[:, a:b]), [(cores[nxt], raw(T["lq%d" % r][:, a:b]))], to_next, "aa%d" % r)

    def scores(r, p):
        a, b = cuts(r)[p:p + 2]
        qx, sx = T["qx%d" % r], T["sx%d" % r]
        if r == R:
            return mm(2 * p, T.vq, T.vs, 0, qx, sx, a, b, ["vq", "qx%d" % p])
        mm(2 * p, T.u2, T.u2s, 0, qx, sx, a, b, ["u2", "u2s", "qx%d" % p])
        mm(2 * p + 1, T.u1, T.u1s, 0, qx, sx, a, b, ["u1", "u1s", "qx%d" % p])
        act(T.s2[:, a:b], bank(2 * p, b - a), ["p%d" % (2 * p)], ["s2%d" % p])

    def vote(r, p):
        a, b = cuts(r)[p:p + 2]
        tt(T.vr[:, a:b], bank(2 * p + 1, b - a), T.s2[:, a:b], A.is_ge, ["s2%d" % p, "p%d" % (2 * p + 1)], ["vr%d" % p])

    def running_sum(r, p):
        a, b = cuts(r)[p:p + 2]
        scan(T.pin[:, a:b], T.d0[:, 0:b - a], T.vr[:, a:b], T.pin[:, a - 1:a] if p else -float(HC), A.mult, A.add,
             ["d0", "vr%d" % p] + (["pin%d" % (p - 1)] if p else []), ["pin%d" % p])

    def turn(r, p):
        a, b = cuts(r)[p:p + 2]
        tr(T.tsn[:, a:b], T.pin[:, a:b], ["pin%d" % p], ["ts%d" % p])

    def y_out(c, q, copy):
        a, b = HALVES[c:c + 2]
        copy(T.ysb[:, a:b], bank(2 * c, HC), ["p%d" % (2 * c)], ["y%d" % c])
        dma(q, T.y[:, a:b], T.ysb[:, a:b], ["y%d" % c], [], "dout")

    def of_b(a, b):
        lst = T.lst[:, a // 4:b // 4]
        if a >= K:
            return T.win[:, 0:4 * C].indirect(lst), ["lo"] + tags("x", 0, C)
        return T.win[:].indirect(lst), ["lo", "lp"] + tags("x", 0, C) + tags("d", 0, C)

    def halved(a, b):
        src, rd = of_b((a + HC) % C, (a + HC) % C + b - a)
        act(T.hb[:, 4 * a:4 * b], src, rd, tags("h", a, b), -0.5)

    def z_run(a, b):
        src, rd = of_b(a, b)
        tt(T.zt[:, 4 * a:4 * b], src, T.hb[:, 4 * a:4 * b], A.add, rd + tags("h", a, b), tags("z", a, b))

    def z_32(a, b):
        act(T.z32[:, 4 * a:4 * b], T.zt[:, 4 * a:4 * b], tags("z", a, b), tags("zz", a, b), 32.0)

    def layer(c):
        a, b = HALVES[c:c + 2]
        quant(T.qz, T.sz, a, b, T.zt[:, 4 * a:4 * b], tags("z", a, b), ["qz%d" % c])
        for t in (0, 2, 1, 3):
            mm(4 * c + t, T.wq, T.wp, 128 * t, T.qz, T.sz, a, b, ["w", "qz%d" % c])

    def x_32(t, c):
        a, b = HALVES[c:c + 2]
        tt(T.x32[:, 4 * a + t:4 * b:4], bank(4 * c + t, HC), T.z32[:, 4 * a + t:4 * b:4], A.add,
           tags("zz", a, b, [t]) + ["p%d" % (4 * c + t)], tags("xx", a, b, [t]))

    def new_x(planes, c, on_vector=False):
        a, b = HALVES[c:c + 2]
        sl = slice(4 * a + planes[0], 4 * b, 4 // len(planes))
        if on_vector:
            ts(T.win[:, sl], T.x32[:, sl], 0.03125, A.mult, tags("xx", a, b, planes), tags("x", a, b, planes))
        else:
            act(T.win[:, sl], T.x32[:, sl], tags("xx", a, b, planes), tags("x", a, b, planes), 0.03125)

    pick_u("u2", 8)
    quant_x(0, 0)
    pick_u("u1", 0)
    for p in runs(0):
        if p:
            quant_x(0, p)
        scores(0, p)
    for step, p in ((vote, 0), (running_sum, 0), (vote, 1), (vote, 2), (running_sum, 1), (turn, 0), (running_sum, 2),
                    (turn, 1), (turn, 2)):
        step(0, p)

    for r in range(R):
        qx, sx, lq, ls, sb, lw = [T[n % r] for n in ("qx%d", "sx%d", "lq%d", "ls%d", "sb%d", "lw%d")]
        ahead = cuts(r)[1]
        small = ["ts%d" % p for p in runs(r)]
        for h in range(2):
            upto, own_vote = T.tsn[:, 16 * h:C:32], T.tsn[:, 16 * h + 1:C:32]
            tt(sb[:, 24 + 12 * h:36 + 12 * h], upto, own_vote, A.subtract, small, ["se%d" % h])
            act(sb[:, 12 * h:12 + 12 * h], upto, small, ["si%d" % h])
        sums = ["se0", "se1", "si0", "si1"]
        send(sums, sb[:], [(cores[o], lw[:, 48 * rank:48 * rank + 48]) for o in others], all_mask(rank),
             "av%d%d" % (r, rank))
        whole = ["qx%d" % p for p in runs(r)]
        send(whole, sx[:], [(cores[nxt], ls[:])], to_next, "ap%d" % r)
        send(whole, raw(qx[:, ahead:C]), [(cores[nxt], raw(lq[:, ahead:C]))], to_next, "ab%d" % r)

        if r == 0:
            late_constants()
        if r == 1:
            quant(T.vq, T.vs, 0, 128, T.vt[:], ["vt"], ["vq"])
            affine(T.odf[:], T.nil[:], 1, HC, ["nil"], ["odf"])
            dma("s", T.od[:], T.odf[0:8, :], ["odf"], ["od"], "dod")
        for c, (a, b) in enumerate(((0, ahead), (ahead, C))):
            for t in range(4):
                k = 4 * (1 - c) + t
                mm(k, T.eq, T.es, 128 * t, lq, ls, a, b, ["eq%d" % t, "ls%d" % r, ("lqa%d", "lqb%d")[c] % r])
                act(T.win[:, 4 * (C + a) + t:4 * (C + b):4], bank(k, b - a), ["p%d" % k], tags("d", a, b, [t]))

        def n24(buf, i):
            return buf[:, 24 * i:24 * i + 24]

        def n32(buf, i):
            return buf[:, 32 * i:32 * i + 32]

        def n64(buf, i):
            return buf[:, 64 * i:64 * i + 64]

        def part(buf, slot, sender, i):
            return n24(buf, 2 * slot + (0 if sender < (rank, prev)[i] else 1))

        def landed(m):
            return "lw%d%d" % (r, m)

        def votes_before(m):
            if m == prev:
                tt(n24(T.vo, 1), n24(lw, 2 * m), n24(lw, 2 * m + 1), A.subtract, [landed(m)], ["vo1"])

        tt(n24(T.vo, 0), n24(sb, 0), n24(sb, 1), A.subtract, sums, ["vo0"])
        for i in range(2):
            tt(n24(T.kk, i), n24(T.kc, i), part(sb, 0, rank, i), A.subtract,
               ["kc%d" % (2 * i), "kc%d" % (2 * i + 1)] + sums, ["kk%d" % i])
        for m, src, dst, sn, dn in ((others[0], T.kk, T.w1, "kk%d", "w1%d"), (others[1], T.w1, T.w2, "w1%d", "w2%d")):
            for i in range(2):
                tt(n24(dst, i), n24(src, i), part(lw, m, m, i), A.subtract, [sn % i, landed(m)], [dn % i])
            votes_before(m)

        def signs(i):
            m = others[2]
            tt(n24(T.sg, i), part(lw, m, m, i), n24(T.w2, i), A.is_ge, [landed(m), "w2%d" % i], ["sg%d" % i])
            if i == 0:
                votes_before(m)

        def leaving(i):
            tt(T.tb[:, 64 * i + 32:64 * i + 56], n24(T.sg, i), n24(T.vo, i), A.is_equal, ["sg%d" % i, "vo%d" % i],
               ["tb%d" % (2 * i + 1)])

        def earlier_blocks(i):
            scan(T.tb[:, 64 * i + 1:64 * i + 24], T.tb[:, 64 * i + 32:64 * i + 55], T.m23[:, 0:23], 0.0, A.add, A.mult,
                 ["tb%d" % (2 * i + 1), "m23"], ["tb%d" % (2 * i)])

        def blocks_to_rows(i):
            tr(n64(T.tu, i), n64(T.tb, i), ["tb%d" % (2 * i), "tb%d" % (2 * i + 1)], ["tu%d" % i])

        def counts(i):
            scan(n64(T.sc, i), T.inc[:], n64(T.tu, i), first, A.add, A.subtract, ["inc0", "inc1", "first", "tu%d" % i],
                 ["sc%d" % i])
            tt(n32(T.lm, i), n32(T.tu, 2 * i + 1), T.cj[:], A.mult, ["tu%d" % i, "cj"], ["lm%d" % i])

        def places(i):
            tt(T.pt[:, 64 * i + 16:64 * i + 48], n32(T.sc, 2 * i + 1), n32(T.lm, i), A.add, ["sc%d" % i, "lm%d" % i],
               ["pt%d" % i])

        def rows_to_groups(i):
            tr(T.tw[:, 96 * i:96 * i + 64], n64(T.pt, i), ["pt%d" % i], ["twa%d" % i])
            tr(T.tw[:, 96 * i + 64:96 * i + 96], T.pt[:, 64 * i + 16:64 * i + 48], ["pt%d" % i], ["twb%d" % i])

        def offsets(i):
            ts(n32(T.offs, i), T.tw[:, 96 * i:96 * i + 96].indirect(T.so[:]), float(HC), A.add,
               ["twa%d" % i, "twb%d" % i, "so0", "so1"], ["offs%d" % i])

        for step in (signs, leaving, earlier_blocks, blocks_to_rows, counts, places, rows_to_groups, offsets):
            step(0)
            step(1)

        def scatter_before(a, b):
            cp(T.npv[:].indirect(T.offs[:, 32 + a // 16:32 + b // 16]), T.vals[:, a:b], ["offs1", "vals"], ["npv"])

        cp(T.no[:].indirect(T.offs[:, 0:24]), T.vals[:], ["offs0", "vals"], ["no"])
        if r == R - 1:
            op("g", lambda: g.dma_start(T.od[:], T.no[0:128:16, :], accum_op=A.add), ["no", "od"], (), "dadd", 16)
        scatter_before(0, 32)
        scan(T.dg[:, 0:C - K], T.no[:, 0:C - K], T.hold[:], BIG, A.min, A.add, ["no", "hold"], ["dg0"])
        ts(T.lst[:, K // 4:QC], T.dg[:, 3:C - K:4], 4.0, A.mult, ["dg0", "el0"], ["lo"], T.el[:, 0:1], A.add)
        halved(HC + K, C)
        halved(0, QC)
        halved(QC, HC)
        scatter_before(32, C)
        z_run(C - 32, C - 24)
        scan(T.dg[:, C - K:C], T.npv[:, C - K:C], T.hold[:, 0:K], BIG, A.min, A.add, ["npv", "hold"], ["dg1"])
        z_run(C - 24, C - 8)
        ts(T.lst[:, 0:K // 4], T.dg[:, C - K + 3:C:4], 4.0, A.mult, ["dg1", "el1"], ["lp"], T.el[:, 1:2], A.add)
        z_run(C - 8, C)

        mid = HC + K // 2
        halved(HC, mid)
        halved(mid, HC + K)
        z_run(0, QC)
        z_run(QC, HC)
        z_32(0, HC)
        z_run(HC, mid)
        layer(0)
        z_run(mid, HC + K)
        z_32(HC, mid)
        z_32(mid, C)
        for c in range(2):
            for t in (0, 2, 1, 3):
                x_32(t, c)
                if (t, c) == (0, 0):
                    layer(1)
                if (t, c) == (3, 1):
                    quant_x(r + 1, 0)
                    scores(r + 1, 0)
                if t == 2 or (t, c) == (3, 0):
                    new_x((t - 2, t), c)
                elif t and c:
                    new_x((t,), c, t == 3)
        if r + 1 < R:
            quant_x(r + 1, 1)
            scores(r + 1, 1)
            for step, p in ((vote, 0), (running_sum, 0), (vote, 1), (turn, 0), (running_sum, 1), (turn, 1)):
                step(r + 1, p)

    y_out(0, "s", act)
    quant_x(R, 1)
    scores(R, 1)
    for k in range(4):
        dma("s" if k else "y", T.osc[4 * k:4 * k + 4, :], T["sx%d" % R][32 * k:32 * k + 4, :], ["qx0", "qx1"], [], "dout")
    y_out(1, "y", cp)
    for sem, val in count.items():
        wait("g", (sem, val, {}))
